import numpy as np, ml_dtypes
CORES = [35,38,43,46]
N = 4
import mx_ref
BF = ml_dtypes.bfloat16
def gcols(t, e):
    v = np.concatenate([t.reshape(8, 16, -1, 4), np.zeros((8, 16, 1, 4), BF)], axis=2)
    return np.ascontiguousarray(np.stack([v[g][:, e[g]] for g in range(8)])).reshape(128, -1)
def tile(rs):
    return np.stack(rs, axis=2).reshape(128, -1).astype(BF)
def cut(t, i, w=512):
    return t[:, w * i:w * i + w]
def pick(q, e):
    c = np.concatenate([q[0].reshape(128, -1, 4), np.zeros((128, 1, 4), np.uint8)], axis=1); s = np.concatenate([q[1], np.ones((16, 1), np.uint8)], axis=1)
    return (np.ascontiguousarray(c[:, e].reshape(128, -1)), np.ascontiguousarray(s[:, e]))
def join(*qs):
    return (np.concatenate([q[0] for q in qs], axis=1), np.concatenate([q[1] for q in qs], axis=1))
def put(q, e, v):
    c, s = q[0].reshape(128, -1, 4).copy(), q[1].copy(); c[:, e] = v[0].reshape(128, -1, 4); s[:, e] = v[1]
    return (c.reshape(128, -1), s)
def pk(c, s):
    return (np.ascontiguousarray(c), mx_ref.live(s))
def emit(q):
    return q[0], q[1]
def packed(v, rng):
    q = [mx_ref.quantize(np.ascontiguousarray(v[r])) for r in range(N)]
    return np.stack([a for a, b in q]), np.stack([mx_ref.plane(b, rng) for a, b in q])
def values_of_codes():
    e, c = np.zeros((128, 128, 4), np.float32), np.zeros((128, 2, 4), np.uint8)
    e[np.arange(128), np.arange(128), 0] = 1
    c[:127, :, 0] = np.arange(256).reshape(2, 128).T[:127]
    return mx_ref.matmul(mx_ref.quantize(e.reshape(128, 512).astype(BF)), (c.reshape(128, 8), np.full((16, 2), 127, np.uint8))).T.reshape(-1).astype(np.float64)
CODE_VALUE, SCALE_VALUE = values_of_codes(), 2.0 ** (np.arange(256) - 127.0)
def decode(q):
    return (CODE_VALUE[q[0]].reshape(16, 8, -1, 4) * SCALE_VALUE[q[1]][:, None, :, None] + 0.0).reshape(128, -1).astype(np.float32)
def f(rng, *shape):
    return mx_ref.flush((rng.standard_normal(shape, dtype=np.float32) * np.exp2(rng.integers(-2, 3, shape[:-1] + (1,)))).astype(BF))
def wide(rng, *shape, cols=0):
    v = rng.standard_normal(shape, dtype=np.float32) * np.exp2(rng.integers(-12, 13, shape)).astype(np.float32)
    if cols: v *= np.repeat(np.exp2(rng.integers(-cols, cols + 1, shape[:-2] + (1, shape[-1] // 4))) * (rng.random(shape[:-2] + (1, shape[-1] // 4)) > 0.0625), 4, axis=-1).astype(np.float32)
    return mx_ref.flush(v.astype(BF))
C, A, R = 384, 240, 3
def slots(s, p):
    b = s[1] > s[0]
    late = np.where(b, s[1] > p[1], s[0] > p[0])
    c = np.sort(np.where(late, C * b + np.arange(C), 2 * C), axis=1)[:, :A]
    return np.where(c < 2 * C, c, -1)
def replaced(t, e, v):
    p = np.tile(np.arange(C + 1), (8, 1))
    p[np.arange(8)[:, None], e] = C + np.arange(A)
    return gcols(np.concatenate([t, v], axis=1), p[:, :C])
def big(v, k):
    v = v.astype(np.float32) * np.float32(k)
    v[np.abs(v) < np.float32(2.0 ** -16)] = 0
    return v.astype(BF)
def weights(rng, w):
    c, p = packed(w, rng)
    return {"wc": c, "ws": p}
def numbers_of(rng):
    return {"x": big(f(rng, N, 128, 12 * C), 1), "u": np.array(f(rng, N, 128, 512)), "v": np.array(f(rng, N, 128, 512))}
def kinds(rng):
    one = [(A, 0), (A - 1, 1), (A - 1, 2), (0, A), (0, A + 1), (1, 0), (0, 0), (C // 2, C - C // 2)]
    two = [(C, 0), (0, C), (A + 1, 0), (A - 1, 0), (0, A - 1), (0, 1), (C - 1, 1), (1, C - 1)]
    n = np.zeros((N, 8, 2), int)
    o = rng.permutation(N)
    for r in range(N):
        if o[r] > 0: n[r] = rng.permutation(np.array(two if o[r] == 1 else one))
    p = np.argsort(rng.random((N, 8, C)), axis=2)
    return (p >= n[:, :, :1]).astype(int) + (p >= n[:, :, :1] + n[:, :, 1:]).astype(int)
def marks(rng):
    c = kinds(rng)
    after = np.roll(c, -1, axis=0)
    m = np.full((N, 8, 3, C), 2)
    m[:, :, 0] = np.where(c == 0, 1, np.where(c == 1, rng.integers(1, 4, c.shape), rng.integers(2, 4, c.shape)))
    m[:, :, 2] = np.where(after == 1, 3, rng.integers(1, 3, c.shape))
    return m
def passing(rng):
    w = big(f(rng, N, 128, 2048), 1).reshape(N, 8, 16, 4, 8, 16, 4)
    w[:, :, 0] = 0
    w[:, :, 8:] = 0
    w[:, :, :, :, :, 0] = 0
    w[:, :, :, :, :, 8:] = 0
    w = w.reshape(N, 128, 4, 128, 4)
    for i in range(0, 128, 8):
        for b in range(4): w[:, i, b, i, b] = 32
    return weights(rng, w.reshape(N, 128, 2048))
def requantised():
    v = (np.arange(1, 16, 2)[:, None] * 2.0 ** -np.arange(10.0, 22.0)).reshape(-1)
    t = np.zeros((128, len(v), 4), np.float32)
    t[8, :, 0] = v
    t[9, :, 0] = 255 * 2.0 ** -7
    once = decode(mx_ref.quantize(t.reshape(128, -1).astype(BF)))
    again = decode(mx_ref.quantize(once.astype(BF)))
    i = int(np.argmax(np.abs(once - again)[8, ::4]))
    return float(v[i]), float(once[8, 4 * i]), float(again[8, 4 * i])
def planted(rng, m, unit, near, fine=False):
    d = numbers_of(rng)
    p = rng.permutation(8)
    s = p % 2 * 2 - 1
    if not near: m = np.where(s[:, None, None] > 0, m, 4 - m)
    x = d["x"].reshape(N, 8, 16, 3, C, 4)
    x[:, :, 0] = 0
    x[:, :, 8:] = 0
    x[:, :, 0, :, :, 0] = near
    if near: x[:, :, 0, 0, :, 0] = np.where(np.roll(m[:, :, 2], 1, axis=0) == 3, s[:, None] * 2.0 ** 28, 1.0).astype(np.float32).astype(BF)
    for b in range(3): x[:, :, 8, :, :, b] = ((m >> b & 1) * 2.0 ** b * unit).astype(np.float32).astype(BF)
    if fine:
        for g in range(8):
            if p[g] < 4:
                x[:, g, 8] = 0
                x[:, g, 8, :, :, 0] = ((4 + m[:, g]) * 2.0 ** -32).astype(np.float32).astype(BF)
        v, once, again = requantised()
        for h in (5, 7):
            g, j = int(np.argmax(p == h)), int(rng.integers(A))
            x[:, g, 8, :, j] = 0
            x[:, g, 8, 0, j, 0] = BF(min(once, again))
            x[:, g, 8, 1, j, 0] = BF(v)
            x[:, g, 9, 1, j, 0] = BF(255 * 2.0 ** -7)
    u = d["u"].reshape(N, 128, 128, 4)
    u[:, :, ::16] = 0
    k = np.where(rng.permutation(N) < N // 2, 2.0 ** -30, 1.0)
    for g in range(8):
        u[:, 16 * g, 16 * g, 0] = (k * s[g]).astype(np.float32).astype(BF)
        u[:, 16 * g + 8, 16 * g, :3] = (k * (1 if near else s[g])).astype(np.float32).astype(BF)[:, None]
    return {"x": x.reshape(N, 128, 12 * C), "u": u.reshape(N, 128, 512), "v": d["v"], **passing(rng)}
def setup_inputs(rng):
    return {**numbers_of(rng), **weights(rng, f(rng, N, 128, 2048))}
def setup_inputs_counts(rng):
    return planted(rng, marks(rng), 1.0, 0)
def setup_inputs_ties(rng):
    return planted(rng, rng.integers(0, 4, (N, 8, 3, C)), 2.0 ** -24, 0, True)
def setup_inputs_near(rng):
    return planted(rng, marks(rng), 2.0 ** -23, 1)
def setup_inputs_huge(rng):
    d = numbers_of(rng)
    x = 2.0 ** 28 * (1.5 + 0.5 * rng.random((N, 128, 12 * C)))
    x[int(rng.integers(N))] *= 2
    u = d["u"].reshape(N, 128, 128, 4)
    s = np.stack([rng.permutation(8) % 2 * 2.0 - 1.0 for r in range(N)])
    u[:, :, ::16] = (2.0 ** 30 * (0.75 + 0.25 * rng.random((N, 128, 8, 4))) * s[:, None, :, None]).astype(np.float32).astype(BF)
    w = np.zeros((N, 128, 4, 128, 4), np.float32)
    i = np.arange(128)
    for b in range(4): w[:, i, b, i, b] = 32
    return {"x": x.astype(np.float32).astype(BF), "u": u.reshape(N, 128, 512), "v": d["v"], **weights(rng, w.reshape(N, 128, 2048).astype(BF))}
def setup_inputs_spread(rng):
    d = setup_inputs(rng)
    d["x"] = big(wide(rng, N, 128, 12 * C, cols=6), 1)
    return d
def check_inputs(d):
    b = []
    for k in ("x", "u", "v"):
        a = np.abs(d[k].astype(np.float32))
        if not (np.isfinite(a).all() and ((a == 0) | (a >= 2.0 ** -30) & (a <= 2.0 ** 30)).all()): b.append("a value of " + k)
    return b
def reference(x, u, v, wc, ws):
    lay = [pk(wc[r], ws[r]) for r in range(N)]
    qu = [mx_ref.quantize(u[r]) for r in range(N)]
    level = [[np.ascontiguousarray(cut(x[r], k, 4 * C)) for k in range(3)] for r in range(N)]
    first = [mx_ref.matmul(qu[r], mx_ref.quantize(level[r][0]))[::16] for r in range(N)]
    y, ol = np.zeros((N, 128, C), np.float32), np.zeros((N, 8, R * A), np.float32)
    oc, osc = np.zeros((N, 128, 4 * C), np.uint8), np.zeros((N, 16, C), np.uint8)
    for t in range(R):
        held = [[mx_ref.quantize(level[r][k]) for k in (1, 2)] for r in range(N)]
        for r in range(N):
            log = [decode(q).astype(BF) for q in held[(r - 1) % N]]
            s = [mx_ref.matmul(qu[r], mx_ref.quantize(g))[::16] for g in log]
            p = [first[r], mx_ref.matmul(qu[r], held[r][0])[::16]]
            c = slots(s, p)
            ol[r][:, A * t:A * t + A] = c
            e = np.where(c < 0, -1, c % C)
            for k in (0, 1):
                z = (gcols(level[r][k], e).astype(np.float32) + gcols(log[k], e).astype(np.float32)) * np.float32(0.5)
                q = mx_ref.quantize(z.astype(BF))
                made = tile([np.maximum(mx_ref.matmul(pick(lay[r], np.arange(128 * a, 128 * a + 128)), q), np.float32(0.0)) * np.float32(0.03125) for a in range(4)])
                level[r][k + 1] = replaced(level[r][k + 1], np.where(c < C * k + C, e, -1), made)
    for r in range(N):
        q = mx_ref.quantize(level[r][2])
        y[r] = mx_ref.matmul(mx_ref.quantize(v[r]), q)
        oc[r], osc[r] = emit(q)
    return {"y": y, "ol": ol, "oc": oc, "osc": osc}

@@ -1,0 +1,415 @@
+from concourse.mybir import dt, AluOpType as ALU, ActivationFunctionType as ACT
+
+C, A, R = 384, 240, 3
+SEC = 256
+PL = C + R * SEC
+KS = [2 * (C + 16), 2 * (C + 16 + SEC), 2 * (C + 16)]
+LW = C + 2 * A
+EMPTY = -1524.0
+STEP = 4096.0
+BF, F32, I32, U16, F16 = "bfloat16", "float32", "int32", "uint16", "float16"
+CODE, PLANE = "float8_e4m3fn_x4", "uint8"
+NS = 2 * C + 4 * A
+CZ, CB = 34, 32
+
+SCRATCH = {"acc": ("psum", [128, 4096], F32)}
+
+
+def _buf(dtype, **sizes):
+    for name, n in sizes.items():
+        SCRATCH[name] = ("sbuf", [128, n], dtype)
+
+
+for _n, _w in (("s", NS), ("l", NS), ("g0", C), ("g1", C), ("z0", A), ("z1", A), ("h0", C), ("h1", C), ("u", 128),
+               ("up", 128), ("v", 128), ("e", 512), ("w", 512), ("f", C)):
+    _buf(CODE, **{"q" + _n: _w})
+    _buf(PLANE, **{"c" + _n: _w})
+_buf(BF, gw0=16 + 8 * C, gw1=16 + 8 * C, gw2=16 + 8 * C, m0=16 + 4 * C, g0=16 + 4 * C)
+_buf(BF, g00=4 * C, gp0=4 * PL, gp1=4 * PL, h2=4 * C, h2p=4 * PL, t1=4 * A, h2f=4 * C, h1p=4 * PL, t0=4 * A)
+_buf(BF, z0=4 * A, z1=4 * A, zb=4 * A, ub=512, vb=512, et=2048, fl=2 * C + 2, junk=C)
+_buf(I32, rampi=C, pci=8, modi=C, mod4=A, vi=48, par=48)
+_buf(F16, a1=4 * C, cnt=2 * C, held=2 * C)
+_buf(F32, lw0=LW, lw1=LW, lw2=LW, ramp=C, pcf=8, a2=A, val=C, icat=76, ramph=A, jk=48, pe=C, p0=C, p1=C, mm=C, nn=C)
+_buf(F32, yw=72, ow=24, h2o=300, n0=1, sg=76, xs=76, vb2=76, cand=48, cand2=24, src=48, sgo=A, ola=R * A, olb=R * A, yb=C)
+_buf(U16, offu=8, offs=24, offz=60, offb=76, srcu=96, lland=96, offf=24)
+
+SEMAPHORES = (["nv", "ns", "nt", "ng", "sent0", "sent"] + ["arr%d" % i for i in range(8)]
+              + ["d%d" % i for i in range(32)])
+
+
+def rank_program(g, core, T, topo):
+    rank = T.rank_of(core)
+    if rank is None:
+        return
+    cores = T.cores
+    nxt, prv = cores[(rank + 1) % len(cores)], cores[(rank - 1) % len(cores)]
+    rid, pid = topo.addr(nxt)[:2]
+    mask = topo.mask(core, nxt)
+    n_out, n_in = len(topo.engines(core, nxt)), len(topo.engines(prv, core))
+    Q = {"v": g.vector, "s": g.scalar, "t": g.tensor, "g": g, "y": g.sync}
+    total, waited, seen, dmas = {}, {k: {} for k in Q}, {}, [0]
+
+    def r(name, lo=0, hi=None, step=1):
+        return (name, lo, SCRATCH[name][1][1] if hi is None else hi, step)
+
+    def ap(x):
+        return T[x[0]][:, x[1]:x[2]:x[3]] if x[3] > 1 else T[x[0]][:, x[1]:x[2]]
+
+    def bank(b, n):
+        return ("acc", 512 * b, 512 * b + n, 1)
+
+    def meet(a, b):
+        if a[0] == "acc":
+            return a[1] // 512 == b[1] // 512
+        if a[2] <= b[1] or b[2] <= a[1]:
+            return False
+        return not (a[3] > 1 and a[3] == b[3] and a[1] % a[3] != b[1] % b[3])
+
+    def wait(q, toks):
+        need = {}
+        for s, n in toks:
+            need[s] = max(need.get(s, 0), n)
+        for s, n in need.items():
+            if waited[q].get(s, 0) < n:
+                Q[q].wait_ge(T.sem[s], n)
+                waited[q][s] = n
+
+    def before(q, reads, writes, after):
+        toks = list(after)
+        for x, wr in [(x, False) for x in reads] + [(x, True) for x in writes]:
+            for y, ywr, yq, tok in seen.get(x[0], []):
+                if meet(x, y) and (wr or ywr or (x[0] == "acc" and yq != q)):
+                    toks.append(tok)
+        wait(q, toks)
+
+    def note(q, reads, writes, tok):
+        for x in reads:
+            seen.setdefault(x[0], []).append((x, False, q, tok))
+        for x in writes:
+            seen.setdefault(x[0], []).append((x, True, q, tok))
+        return tok
+
+    def op(q, call, reads, writes, after=()):
+        before(q, reads, writes, after)
+        s = "n" + q
+        call().then_inc(T.sem[s], 1)
+        total[s] = total.get(s, 0) + 1
+        return note(q, reads, writes, (s, total[s]))
+
+    def dma(q, out, in_, reads, writes, after=(), **kw):
+        before(q, reads, writes, after)
+        s = "d%d" % dmas[0]
+        dmas[0] += 1
+        Q[q].dma_start(out, in_, **kw).then_inc(T.sem[s], 16)
+        total[s] = 16
+        return note(q, reads, writes, (s, 16))
+
+    def send(src, dst, arr, local, bits):
+        before("g", [src], [], ())
+        a, b = ap(src), ap(dst)
+        if bits:
+            a, b = a.bitcast(dt.uint8), b.bitcast(dt.uint8)
+        g.remote_dma(b, a, T.sem[arr], T.sem[local], pid, rid, mask)
+        total[local] = total.get(local, 0) + n_out
+
+    def arrives(regions, arr, calls):
+        total[arr] = calls * n_in
+        note("x", [], regions, (arr, calls * n_in))
+
+    def send_pair(lo, n, arr, local):
+        send(r("qs", lo, lo + n), r("ql", lo, lo + n), arr, local, True)
+        send(r("cs", lo, lo + n), r("cl", lo, lo + n), arr, local, False)
+        arrives([r("ql", lo, lo + n), r("cl", lo, lo + n)], arr, 2)
+
+    def quant(name, lo, n, src):
+        c, s = r("q" + name, lo, lo + n), r("c" + name, lo, lo + n)
+        return op("v", lambda: g.vector.quantize_mx(ap(c), ap(s), ap(src)), [src], [c, s])
+
+    def mm(b, wn, wlo, xn, xlo, n):
+        wc, ws = r("q" + wn, wlo, wlo + 128), r("c" + wn, wlo, wlo + 128)
+        xc, xs = r("q" + xn, xlo, xlo + n), r("c" + xn, xlo, xlo + n)
+        o = bank(b, n)
+        return op("t", lambda: g.tensor.matmul_mx(ap(o), ap(wc), ap(ws), ap(xc), ap(xs), True, True),
+                  [wc, ws, xc, xs], [o])
+
+    def src_ap(x, off):
+        return ap(x) if off is None else ap(x).indirect(ap(off))
+
+    def ts(out, in0, s1, op0, s2=None, op1=None, off=None):
+        reads = [in0] + [s for s in (s1, s2, off) if isinstance(s, tuple)]
+        a1 = ap(s1) if isinstance(s1, tuple) else s1
+        a2 = ap(s2) if isinstance(s2, tuple) else s2
+        if op1 is None:
+            return op("v", lambda: g.vector.tensor_scalar(ap(out), src_ap(in0, off), a1, None, op0), reads, [out])
+        return op("v", lambda: g.vector.tensor_scalar(ap(out), src_ap(in0, off), a1, a2, op0, op1), reads, [out])
+
+    def tt(out, in0, in1, o, off=None):
+        return op("v", lambda: g.vector.tensor_tensor(ap(out), src_ap(in0, off), ap(in1), o),
+                  [in0, in1] + ([off] if off else []), [out])
+
+    def cp(out, in_, off=None):
+        return op("v", lambda: g.vector.tensor_copy(ap(out), src_ap(in_, off)), [in_] + ([off] if off else []), [out])
+
+    def scan(out, d0, d1, init, op0, op1):
+        return op("v", lambda: g.vector.tensor_tensor_scan(ap(out), ap(d0), ap(d1), init, op0, op1), [d0, d1], [out])
+
+    def act(out, in_, func, scale=None, bias=None, off=None, acc=None):
+        kw = {}
+        if scale is not None:
+            kw["scale"] = scale
+        if bias is not None:
+            kw["bias"] = ap(bias) if isinstance(bias, tuple) else bias
+        if acc is not None:
+            kw["accum_out"] = ap(acc)
+        reads = [in_] + [s for s in (bias, off) if isinstance(s, tuple)]
+        return op("s", lambda: g.scalar.activation(ap(out), src_ap(in_, off), func, **kw), reads,
+                  [out] + ([acc] if acc else []))
+
+    def move(q, out, in_, off=None, scale=None):
+        if q == "s":
+            return act(out, in_, ACT.Copy, scale=scale, off=off)
+        if scale is None:
+            return cp(out, in_, off)
+        return ts(out, in_, scale, ALU.mult, off=off)
+
+    def relu(q, out, b, scale):
+        if q == "s":
+            return act(out, bank(b, A), ACT.Relu, scale=scale)
+        return ts(out, bank(b, A), 0.0, ALU.max, scale, ALU.mult)
+
+    def col(i):
+        return r("pcf", i, i + 1)
+
+    def tq(t, k):
+        return 2 * C + A * (2 * t + k)
+
+    gw = ["gw0", "gw1", "gw2"]
+    G1 = 16 + 4 * C
+    half = C // 2
+
+    def h1(t):
+        return r(gw[t], 16, 16 + 4 * C)
+
+    def log(k, t, a=None):
+        name, lo = (gw[t], G1) if k else (("g0", 16) if t else ("g00", 0))
+        return r(name, lo, lo + 4 * C) if a is None else r(name, lo + a, lo + 4 * C, 4)
+
+    def tsec(t):
+        return C + 16 + SEC * t
+
+    def planes(name, lo, src, n, scale=None):
+        for a in range(4):
+            act(r(name, a * PL + lo, a * PL + lo + n), r(src[0], src[1] + a, src[2], 4), ACT.Copy, scale=scale)
+
+    def hold_pattern(i):
+        ts(r("a1", 2 * C * i, 2 * C * i + C), r("modi"), col(1), ALU.is_le, float(KS[i] + 2 * A), ALU.mult)
+        cp(r("a1", 2 * C * i + C, 2 * C * i + 2 * C), r("a1", 2 * C * i, 2 * C * i + C))
+
+    def zero(name, lo, n):
+        act(r(name, lo, lo + n), r("ramp", 0, n), ACT.Copy, scale=0.0)
+
+    for i in range(2):
+        part = r("gw0", 16 + 4 * half * i, 16 + 4 * half * (i + 1))
+        dma("y", ap(part), T.x[:, 4 * C + 4 * half * i:4 * C + 4 * half * (i + 1)], [], [part])
+    dma("y", ap(r("h2")), T.x[:, 8 * C:12 * C], [], [r("h2")])
+    dma("y", ap(r("ub")), T.u[:], [], [r("ub")])
+    dma("y", ap(r("m0", 16)), T.x[:, 0:4 * C], [], [r("m0", 16)])
+
+    op("g", lambda: g.iota(ap(r("pci", 0, 1)), [[1, 1]], 0, 1), [], [r("pci", 0, 1)])
+    op("g", lambda: g.iota(ap(r("ramp")), [[1, C]], 0, 0, allow_small_or_imprecise_dtypes=True), [], [r("ramp")])
+    op("g", lambda: g.iota(ap(r("rampi")), [[1, C]], 0, 0), [], [r("rampi")])
+    op("v", lambda: g.vector.memset(ap(r("et")), 0.0), [], [r("et")])
+    cp(col(0), r("pci", 0, 1))
+    ts(r("pci", 1, 2), r("pci", 0, 1), 15, ALU.bitwise_and)
+    ts(r("pci", 2, 3), r("pci", 0, 1), 3, ALU.bitwise_and)
+    for b in range(4):
+        ts(r("et", 513 * b, 512 * b + 512, 4), r("ramp", 0, 128), col(0), ALU.is_equal)
+    ts(r("pci", 3, 4), r("pci", 1, 2), 2, ALU.logical_shift_right)
+    cp(col(1), r("pci", 1, 2))
+    ts(col(2), r("pci", 2, 3), 16.0, ALU.add)
+    ts(col(3), r("pci", 3, 4), 0.5, ALU.add)
+    ts(col(4), r("pci", 3, 4), -STEP, ALU.mult, 3 * STEP, ALU.add)
+    ts(col(5), r("pci", 3, 4), -STEP, ALU.mult, 3 * STEP - 768.0, ALU.add)
+    ts(col(6), r("pci", 3, 4), -STEP, ALU.mult, 3 * STEP - 1520.0, ALU.add)
+    cp(r("offu"), r("ramp", 0, 128, 16))
+    for t in range(R):
+        act(r("lw%d" % t, C + 1, LW, 2), r("ramp", 0, A), ACT.Identity, scale=0.0, bias=EMPTY)
+        for a in range(4):
+            zero("h1p", a * PL + tsec(t) - 16, 16)
+        zero(gw[t], 0, 16)
+    zero("m0", 0, 16)
+    zero("g0", 0, 16)
+    zero("fl", 0, 2)
+    for i in range(2):
+        quant("s", half * i, half, r("gw0", 16 + 4 * half * i, 16 + 4 * half * (i + 1)))
+        send(r("qs", half * i, half * (i + 1)), r("ql", half * i, half * (i + 1)), "arr0", "sent0", True)
+    send(r("cs", 0, C), r("cl", 0, C), "arr0", "sent0", False)
+    arrives([r("ql", 0, C), r("cl", 0, C)], "arr0", 3)
+    quant("s", C, C, r("h2"))
+    send_pair(C, C, "arr1", "sent0")
+    first_sent = ("sent0", total["sent0"])
+    quant("e", 0, 512, r("et"))
+    planes("h1p", 0, h1(0), C, 0.5)
+    planes("h2p", 0, r("h2"), C)
+    quant("u", 0, 128, r("ub"))
+    op("v", lambda: g.vector.tensor_copy(T.qup[:, 0:128].bitcast(dt.uint32),
+                                         T.qu[:, 0:128].bitcast(dt.uint32).indirect(T.offu[:, 0:8])),
+       [r("qu"), r("offu")], [r("qup")])
+    op("v", lambda: g.vector.tensor_copy(T.cup[:, 0:128], T.cu[:, 0:128].indirect(T.offu[:, 0:8])),
+       [r("cu"), r("offu")], [r("cup")])
+    quant("h0", 0, C, r("m0", 16))
+    mm(2, "up", 0, "h0", 0, C)
+    mm(3, "up", 0, "s", 0, C)
+    act(r("pe"), bank(2, C), ACT.Abs, scale=2.0 ** -24 + 2.0 ** -30)
+    act(r("pe"), r("pe"), ACT.Identity, bias=2.0 ** -122)
+    act(r("p1"), bank(3, C), ACT.Copy)
+    dma("y", T.qw[:, 0:512].bitcast(dt.uint8), T.wc[:, 0:2048], [], [r("qw")], [first_sent])
+    dma("y", T.cw[:, 0:512], T.ws[:, 0:512], [], [r("cw")])
+    dma("y", ap(r("vb")), T.v[:], [], [r("vb")])
+    ts(r("modi"), r("rampi"), 15, ALU.bitwise_and)
+    ts(r("mod4"), r("rampi", 0, A), 3, ALU.bitwise_and)
+    hold_pattern(0)
+    hold_pattern(1)
+    tt(r("p0"), bank(2, C), r("pe"), ALU.add)
+    ts(r("a2"), r("mod4"), col(3), ALU.is_gt, 2.0 ** 20 + STEP, ALU.mult)
+    for i in range(2):
+        act(r("src", 24 * i, 24 * i + 24), r("ramp", 0, C, 16), ACT.Identity, bias=col(1))
+    for i in range(2):
+        act(r("jk", 24 * i, 24 * i + 24), r("src", 0, 24), ACT.Identity, bias=float(KS[i] - C))
+    act(r("val"), r("ramp"), ACT.Identity, scale=4.0, bias=col(2))
+    act(r("icat", 0, 60), r("ramp", 0, A, 4), ACT.Identity, bias=col(3))
+    act(r("icat", 60, 75), r("src", 0, 15), ACT.Identity, bias=0.5)
+    act(r("h2o", A + 3, 300, 4), r("src", 0, 15), ACT.Identity, bias=col(6))
+    act(r("ramph"), r("ramp", 0, A), ACT.Identity, bias=0.5)
+    act(r("a2"), r("a2"), ACT.Identity, bias=-2.0 ** 20)
+
+    s0, s1 = bank(4, C), bank(0, C)
+    for t in range(R):
+        m0, lw = ("g0" if t else "m0"), "lw%d" % t
+        ki = t % 2
+
+        for k in range(2):
+            b0 = 4 - 4 * k
+            if t == 0:
+                for b in range(4):
+                    mm(b0 + b, "e", 128 * b, "l", C * k, C)
+                if k:
+                    mm(4, "up", 0, "g0", 0, C)
+                for b in range(4):
+                    move("vs"[b % 2], log(k, 0, b), bank(b0 + b, C))
+            else:
+                gp, lo = "gp%d" % k, tsec(t - 1)
+                for b in range(4):
+                    mm(b0 + b, "e", 128 * b, "l", tq(t - 1, k), A)
+                if k:
+                    mm(4, "up", 0, "g0", 0, C)
+                for b in range(4):
+                    move(("vsvs", "vsss")[k][b], r(gp, b * PL + lo, b * PL + lo + A), bank(b0 + b, A))
+                o = 48 * (t - 1) + 24 * (1 - k)
+                for a in range(4):
+                    move("vs"[a % 2], log(k, t, a), r(gp, a * PL, a * PL + lo + A), off=r("lland", o, o + 24))
+            if k or t == 0:
+                sum_in = h1(t) if k else r(m0, 16)
+                dma("g", ap(sum_in), ap(log(k, t)), [log(k, t)], [sum_in], accum_op=ALU.add)
+            quant("g%d" % k, 0, C, log(k, t))
+            if t and not k:
+                dma("g", ap(log(0, t)), T.x[:, 0:4 * C], [], [log(0, t)], accum_op=ALU.add)
+        mm(0, "up", 0, "g1", 0, C)
+        if t == 0:
+            planes("gp0", 0, log(0, 0), C)
+        tt(r("mm"), s0, r("p1"), ALU.max)
+        tt(r("nn"), s1, r("p0"), ALU.max)
+
+        tt(r("fl", 2 + C, 2 + 2 * C), s1, r("mm"), ALU.is_gt)
+        tt(r("fl", 2, 2 + C), s0, r("nn"), ALU.is_ge)
+        act(r("junk"), r("fl", 2, 2 + C), ACT.Identity, scale=-1.0, acc=r("n0"))
+        act(r("sg", 0, 75), r("icat", 0, 75), ACT.Sign, bias=r("n0"))
+        act(r("xs", 0, 75), r("sg", 0, 75), ACT.Copy, scale=-768.0)
+        act(r("sgo"), r("ramph"), ACT.Sign, bias=r("n0"))
+        act(r("olb", A * t, A * t + A), r("sgo"), ACT.Copy, scale=192.0)
+        if t == 0:
+            planes("gp1", 0, log(1, 0), C)
+        else:
+            planes("h2p", tsec(t - 1), r("t1"), A)
+        scan(r("cnt"), r("fl", 2, 2 + 2 * C), r("fl", 1, 1 + 2 * C), float(KS[t]), ALU.add, ALU.add)
+        scan(r("held"), r("a1", 2 * C * ki, 2 * C * ki + 2 * C), r("cnt"), 0.0, ALU.max, ALU.min)
+        cp(r("vi"), r("held", 15, 2 * C, 16))
+        ts(r("par"), r("vi"), 1, ALU.bitwise_and)
+        tt(r("yw", 24, 72), r("vi"), r("par"), ALU.mult)
+        tt(r("yw", 0, 24), r("yw", 24, 48), r("yw", 48, 72), ALU.max)
+        tt(r("ow"), r("yw", 0, 24), r("jk", 24 * ki, 24 * ki + 24), ALU.max)
+        ts(r("offs"), r("ow"), float(C - KS[t]), ALU.add)
+        op("v", lambda: g.vector.tensor_copy(ap(r(lw)).indirect(ap(r("offs"))), ap(r("val"))),
+           [r("val"), r("offs")], [r(lw)])
+        scan(r("h2o", 0, A), r("a2"), r(lw, C + 1, LW, 2), 0.0, ALU.add, ALU.max)
+        ts(r("offz"), r("h2o", 3, A, 4), col(4), ALU.subtract, 0.0, ALU.max)
+        move("s", r("z0", 0, 16 * CZ), r(m0), off=r("offz", 0, CZ), scale=0.5)
+        tt(r("vb2", 0, 75), r("h2o", 3, 300, 4), r("xs", 0, 75), ALU.add)
+        move("v", r("z0", 16 * CZ), r(m0), off=r("offz", CZ, 60), scale=0.5)
+        ts(r("offb", 0, 75), r("vb2", 0, 75), col(5), ALU.subtract, 0.0, ALU.max)
+
+        quant("z0", 0, A, r("z0"))
+        for a in range(4):
+            mm(4 + a, "w", 128 * a, "z0", 0, A)
+        bw = r(gw[t], 0, 16 + 8 * C)
+        move("s", r("zb", 0, 16 * CB), bw, off=r("offb", 0, CB), scale=0.5)
+        move("v", r("zb", 16 * CB), bw, off=r("offb", CB, 60), scale=0.5)
+        for a in range(4):
+            relu("s", r("h1p", a * PL + tsec(t), a * PL + tsec(t) + A), 4 + a, 2.0 ** -6)
+        for a in range(4):
+            tt(r("z1", a, 4 * A, 4), r("h1p", a * PL + tsec(t) - 16, a * PL + tsec(t) + A), r("zb", a, 4 * A, 4),
+               ALU.add, off=r("offb", 60, 75))
+        if t < 2:
+            for a in range(4):
+                relu("s", r("t0", a, 4 * A, 4), 4 + a, 2.0 ** -5)
+            quant("s", tq(t, 0), A, r("t0"))
+            send_pair(tq(t, 0), A, "arr%d" % (4 + t), "sent")
+
+        quant("z1", 0, A, r("z1"))
+        for a in range(4):
+            mm(a, "w", 128 * a, "z1", 0, A)
+        ts(r("cand"), r("yw", 0, 48), 0.5, ALU.mult, -0.5, ALU.add)
+        if t < 2:
+            tt(r("src"), r("src"), r("cand"), ALU.max)
+            mine, theirs, arr = r("srcu", 48 * t, 48 * t + 48), r("lland", 48 * t, 48 * t + 48), "arr%d" % (2 + t)
+            cp(mine, r("src"))
+            send(mine, theirs, arr, "sent", False)
+            arrives([theirs], arr, 1)
+        else:
+            ts(r("cand2"), r("yw", 0, 24), 0.0, ALU.is_gt, float(2 * SEC), ALU.mult)
+            act(r("ola", A * t, A * t + A), r(lw, C + 1, LW, 2), ACT.Identity, scale=0.25, bias=188.0)
+            wrote = dma("y", T.ol[:], T.ola[0:128:16, :], [r("ola")], [])
+            dma("g", T.ol[:], T.olb[0:128:16, :], [r("olb")], [], [wrote], accum_op=ALU.add)
+        for a in range(4):
+            made = r("t1", a, 4 * A, 4) if t < 2 else r("h2p", a * PL + tsec(t), a * PL + tsec(t) + A)
+            relu("vs"[a % 2], made, a, 2.0 ** -5)
+            if t == 2 and a == 0:
+                tt(r("cand", 0, 24), r("cand", 0, 24), r("cand2"), ALU.add)
+                tt(r("src", 0, 24), r("src", 0, 24), r("cand", 0, 24), ALU.max)
+                cp(r("offf"), r("src", 0, 24))
+        if t < 2:
+            quant("s", tq(t, 1), A, r("t1"))
+            send_pair(tq(t, 1), A, "arr%d" % (6 + t), "sent")
+            for a in range(4):
+                move("sv"[a % 2], r(gw[t + 1], 16 + a, 16 + 4 * C, 4), r("h1p", a * PL, a * PL + tsec(t) + A),
+                     off=r("srcu", 48 * t + 24, 48 * t + 48), scale=2.0)
+            if t == 0:
+                quant("v", 0, 128, r("vb"))
+            quant("h1", 0, C, h1(t + 1))
+            mm(3, "up", 0, "h1", 0, C)
+            act(r("ola", A * t, A * t + A), r(lw, C + 1, LW, 2), ACT.Identity, scale=0.25, bias=188.0)
+            act(r("p1"), bank(3, C), ACT.Copy)
+
+    for a in range(4):
+        move("vs"[a % 2], r("h2f", a, 4 * C, 4), r("h2p", a * PL, (a + 1) * PL), off=r("offf"))
+    quant("f", 0, C, r("h2f"))
+    mm(4, "v", 0, "f", 0, half)
+    mm(5, "v", 0, "f", half, half)
+    dma("y", T.oc[:, 0:4 * C], T.qf[:, 0:C].bitcast(dt.uint8), [r("qf")], [])
+    for k in range(4):
+        dma("yg"[k % 2], T.osc[4 * k:4 * k + 4, 0:C], T.cf[32 * k:32 * k + 4, 0:C], [r("cf")], [])
+    move("v", r("yb", 0, half), bank(4, half))
+    move("s", r("yb", half, C), bank(5, half))
+    dma("y", T.y[:, 0:half], ap(r("yb", 0, half)), [r("yb", 0, half)], [])
+    dma("s", T.y[:, half:C], ap(r("yb", half, C)), [r("yb", half, C)], [])
+    wait("g", list(total.items()))

@@ -3,14 +3,28 @@ from concourse.mybir import dt, AluOpType as ALU, ActivationFunctionType as ACT
 C, A, R = 384, 240, 3
 SEC = 256
 PL = C + R * SEC
+HP = 16 + C + A
 KS = [2 * (C + 16), 2 * (C + 16 + SEC), 2 * (C + 16)]
 LW = C + 2 * A
 EMPTY = -1524.0
-STEP = 4096.0
+STEP, FAR = 4096.0, 2.0 ** 20
 BF, F32, I32, U16, F16 = "bfloat16", "float32", "int32", "uint16", "float16"
 CODE, PLANE = "float8_e4m3fn_x4", "uint8"
-NS = 2 * C + 4 * A
-CZ, CB = 34, 32
+NS = 4 * C + 4 * A
+CZ = 30
+CB = 34
+HS = 192
+HF = 192
+WHOLE = (False, True)
+
+P1 = 128
+OPEN = "tD0 tD1 vC0 sC1 vC2 sC3 vQ sc0 sc1 tD2 tS vc3 sc2 vq0 sc4 sc5 sc6 sc7 vm vq1 vf0 vf1 sn"
+K0 = "sB0 vB1 sr0 vz0 sr1 vz1 sr2 vz2 sr3 vz3 "
+G1S = " sc0 sc1 va0 sc2 va1 sc3 sa2 va3 vq0 sb0 sb1 sb2 vb3 vm vq1 vf0 vf1"
+RX = K0 + "st0 st1 st2 st3 vu vW vR0 sR1 vR2 sR3 vT sH0 vH1 sH2 vH3 vh tP sp vv tD0 tD1 vC0 sC1 vC2 sC3 vQ tS" + G1S
+RY = K0 + "sH0 sH1 sH2 vW vH3 vh sR0 sR1 sR2 sR3 vT tP sp vv tD0 vC0 sC1 vC2 sC3 vG0 sG1 vG2 sG3 tD1 vQ tS" + G1S
+LAST = K0 + "vW vL"
+END = "sR0 vR1 sR2 vR3 sa0 va1 sa2 va3 sb0 vq0 vb1 sb2 vb3 sy0 vq1 yo0 so1 yo2 so3 vy1"
 
 SCRATCH = {"acc": ("psum", [128, 4096], F32)}
 
@@ -20,18 +34,19 @@ def _buf(dtype, **sizes):
         SCRATCH[name] = ("sbuf", [128, n], dtype)
 
 
-for _n, _w in (("s", NS), ("l", NS), ("g0", C), ("g1", C), ("z0", A), ("z1", A), ("h0", C), ("h1", C), ("u", 128),
+for _n, _w in (("s", NS), ("l", NS), ("g0", C), ("g1", C), ("z0", A), ("z1", A), ("h0", C), ("u", 128),
                ("up", 128), ("v", 128), ("e", 512), ("w", 512), ("f", C)):
     _buf(CODE, **{"q" + _n: _w})
     _buf(PLANE, **{"c" + _n: _w})
-_buf(BF, gw0=16 + 8 * C, gw1=16 + 8 * C, gw2=16 + 8 * C, m0=16 + 4 * C, g0=16 + 4 * C)
-_buf(BF, g00=4 * C, gp0=4 * PL, gp1=4 * PL, h2=4 * C, h2p=4 * PL, t1=4 * A, h2f=4 * C, h1p=4 * PL, t0=4 * A)
-_buf(BF, z0=4 * A, z1=4 * A, zb=4 * A, ub=512, vb=512, et=2048, fl=2 * C + 2, junk=C)
-_buf(I32, rampi=C, pci=8, modi=C, mod4=A, vi=48, par=48)
+_buf(BF, h1=4 * C, g1=16 + 4 * C, m0=16 + 4 * C, g0=16 + 4 * C, g00=4 * C, h2w=4 * PL, h2f=4 * C)
+_buf(BF, gp0=4 * PL, gp1=4 * PL, h1p=4 * HP, t0=4 * A, z0=4 * A, z1=4 * A, zb=4 * A)
+_buf(BF, ub=512, vb=512, et=2048, fl=2 * C + 2, junk=C, modi=C, mod4=A)
+_buf(I32, pci=8, vi=48, par=48)
 _buf(F16, a1=4 * C, cnt=2 * C, held=2 * C)
-_buf(F32, lw0=LW, lw1=LW, lw2=LW, ramp=C, pcf=8, a2=A, val=C, icat=76, ramph=A, jk=48, pe=C, p0=C, p1=C, mm=C, nn=C)
-_buf(F32, yw=72, ow=24, h2o=300, n0=1, sg=76, xs=76, vb2=76, cand=48, cand2=24, src=48, sgo=A, ola=R * A, olb=R * A, yb=C)
-_buf(U16, offu=8, offs=24, offz=60, offb=76, srcu=96, lland=96, offf=24)
+_buf(F32, lw0=LW, lw1=LW, lw2=LW, ramp=C, pcf=8, a2=A, a3=A, val=C, ramph=A, jk=48, pe=C, p0=C, p1=C, mm=C, nn=C)
+_buf(F32, yw=72, ow=24, h4=A, h16=A, n0=1, lane=24, icat=16, tc=16, sg=16, lev=16, e1=16, vb2=16, cand=72, cand2=24)
+_buf(F32, src=72, f4=96, sgo=A, ola=R * A, olb=R * A, yb=C)
+_buf(U16, offu=8, offs=24, offz=60, offb=16, srcu=144, lland=96, offf=96)
 
 SEMAPHORES = (["nv", "ns", "nt", "ng", "sent0", "sent"] + ["arr%d" % i for i in range(8)]
               + ["d%d" % i for i in range(32)])
@@ -46,6 +61,8 @@ def rank_program(g, core, T, topo):
     rid, pid = topo.addr(nxt)[:2]
     mask = topo.mask(core, nxt)
     n_out, n_in = len(topo.engines(core, nxt)), len(topo.engines(prv, core))
+    near_out, near_in = topo.chip(core) == topo.chip(nxt), topo.chip(core) == topo.chip(prv)
+    whole_out, whole_in = WHOLE[near_out], WHOLE[near_in]
     Q = {"v": g.vector, "s": g.scalar, "t": g.tensor, "g": g, "y": g.sync}
     total, waited, seen, dmas = {}, {k: {} for k in Q}, {}, [0]
 
@@ -55,8 +72,8 @@ def rank_program(g, core, T, topo):
     def ap(x):
         return T[x[0]][:, x[1]:x[2]:x[3]] if x[3] > 1 else T[x[0]][:, x[1]:x[2]]
 
-    def bank(b, n):
-        return ("acc", 512 * b, 512 * b + n, 1)
+    def bank(b, n, lo=0):
+        return ("acc", 512 * b + lo, 512 * b + lo + n, 1)
 
     def meet(a, b):
         if a[0] == "acc":
@@ -116,10 +133,10 @@ def rank_program(g, core, T, topo):
         total[arr] = calls * n_in
         note("x", [], regions, (arr, calls * n_in))
 
-    def send_pair(lo, n, arr, local):
-        send(r("qs", lo, lo + n), r("ql", lo, lo + n), arr, local, True)
-        send(r("cs", lo, lo + n), r("cl", lo, lo + n), arr, local, False)
-        arrives([r("ql", lo, lo + n), r("cl", lo, lo + n)], arr, 2)
+    def send_pair(lo, n, arr, land):
+        send(r("qs", lo, lo + n), r("ql", lo, lo + n), arr, "sent", True)
+        send(r("cs", lo, lo + n), r("cl", lo, lo + n), arr, "sent", False)
+        arrives([r("ql", land[0], sum(land)), r("cl", land[0], sum(land))], arr, 2)
 
     def quant(name, lo, n, src):
         c, s = r("q" + name, lo, lo + n), r("c" + name, lo, lo + n)
@@ -177,80 +194,98 @@ def rank_program(g, core, T, topo):
             return act(out, bank(b, A), ACT.Relu, scale=scale)
         return ts(out, bank(b, A), 0.0, ALU.max, scale, ALU.mult)
 
+    def iota(out, pattern):
+        op("g", lambda: g.iota(ap(out), pattern, 0, 0, allow_small_or_imprecise_dtypes=True), [], [out])
+
     def col(i):
         return r("pcf", i, i + 1)
 
-    def tq(t, k):
-        return 2 * C + A * (2 * t + k)
+    def sent_h1(t):
+        return 2 * C + (C + A) * (t - 1) if t else 0
 
-    gw = ["gw0", "gw1", "gw2"]
-    G1 = 16 + 4 * C
-    half = C // 2
+    def sent_t(t, k):
+        return 3 * C + (C + A) * t if k else 4 * C + 2 * A + A * t
 
-    def h1(t):
-        return r(gw[t], 16, 16 + 4 * C)
+    def land(t):
+        return (sent_h1(t), C) if whole_in else (sent_t(t - 1, 0), A)
 
-    def log(k, t, a=None):
-        name, lo = (gw[t], G1) if k else (("g0", 16) if t else ("g00", 0))
-        return r(name, lo, lo + 4 * C) if a is None else r(name, lo + a, lo + 4 * C, 4)
+    def log(k, t, a=None, lo=0, hi=C):
+        name, base = ("g1", 16) if k else (("g0", 16) if t else ("g00", 0))
+        return r(name, base + 4 * lo, base + 4 * hi) if a is None else r(name, base + 4 * lo + a, base + 4 * hi, 4)
 
     def tsec(t):
         return C + 16 + SEC * t
 
-    def planes(name, lo, src, n, scale=None):
+    def planes(name, width, lo, src, n, scale=None):
         for a in range(4):
-            act(r(name, a * PL + lo, a * PL + lo + n), r(src[0], src[1] + a, src[2], 4), ACT.Copy, scale=scale)
+            act(r(name, a * width + lo, a * width + lo + n), r(src[0], src[1] + a, src[2], 4), ACT.Copy, scale=scale)
 
     def hold_pattern(i):
-        ts(r("a1", 2 * C * i, 2 * C * i + C), r("modi"), col(1), ALU.is_le, float(KS[i] + 2 * A), ALU.mult)
-        cp(r("a1", 2 * C * i + C, 2 * C * i + 2 * C), r("a1", 2 * C * i, 2 * C * i + C))
+        for lo in (2 * C * i, 2 * C * i + C):
+            ts(r("a1", lo, lo + C), r("modi"), col(1), ALU.is_le, float(KS[i] + 2 * A), ALU.mult)
 
     def zero(name, lo, n):
         act(r(name, lo, lo + n), r("ramp", 0, n), ACT.Copy, scale=0.0)
 
-    for i in range(2):
-        part = r("gw0", 16 + 4 * half * i, 16 + 4 * half * (i + 1))
-        dma("y", ap(part), T.x[:, 4 * C + 4 * half * i:4 * C + 4 * half * (i + 1)], [], [part])
-    dma("y", ap(r("h2")), T.x[:, 8 * C:12 * C], [], [r("h2")])
+    def slots_out(t):
+        act(r("ola", A * t, A * t + A), r("lw%d" % t, C + 1, LW, 2), ACT.Identity, scale=0.25, bias=188.0)
+
+    pieces = [(0, P1), (P1, C)] if P1 < C else [(0, C)]
+    for lo, hi in pieces:
+        dma("y", ap(r("h1", 4 * lo, 4 * hi)), T.x[:, 4 * (C + lo):4 * (C + hi)], [], [r("h1", 4 * lo, 4 * hi)])
+    dma("y", ap(r("h2w", 0, 4 * C)), T.x[:, 8 * C:12 * C], [], [r("h2w", 0, 4 * C)])
     dma("y", ap(r("ub")), T.u[:], [], [r("ub")])
     dma("y", ap(r("m0", 16)), T.x[:, 0:4 * C], [], [r("m0", 16)])
 
     op("g", lambda: g.iota(ap(r("pci", 0, 1)), [[1, 1]], 0, 1), [], [r("pci", 0, 1)])
-    op("g", lambda: g.iota(ap(r("ramp")), [[1, C]], 0, 0, allow_small_or_imprecise_dtypes=True), [], [r("ramp")])
-    op("g", lambda: g.iota(ap(r("rampi")), [[1, C]], 0, 0), [], [r("rampi")])
+    iota(r("ramp"), [[1, C]])
+    iota(r("modi"), [[0, C // 16], [1, 16]])
+    iota(r("mod4"), [[0, A // 4], [1, 4]])
     op("v", lambda: g.vector.memset(ap(r("et")), 0.0), [], [r("et")])
     cp(col(0), r("pci", 0, 1))
     ts(r("pci", 1, 2), r("pci", 0, 1), 15, ALU.bitwise_and)
     ts(r("pci", 2, 3), r("pci", 0, 1), 3, ALU.bitwise_and)
-    for b in range(4):
-        ts(r("et", 513 * b, 512 * b + 512, 4), r("ramp", 0, 128), col(0), ALU.is_equal)
     ts(r("pci", 3, 4), r("pci", 1, 2), 2, ALU.logical_shift_right)
     cp(col(1), r("pci", 1, 2))
     ts(col(2), r("pci", 2, 3), 16.0, ALU.add)
     ts(col(3), r("pci", 3, 4), 0.5, ALU.add)
+    for lo, hi in pieces:
+        quant("s", lo, hi - lo, r("h1", 4 * lo, 4 * hi))
+        send(r("qs", lo, hi), r("ql", lo, hi), "arr0", "sent0", True)
+        if lo == 0:
+            for b in range(4):
+                ts(r("et", 513 * b, 512 * b + 512, 4), r("ramp", 0, 128), col(0), ALU.is_equal)
     ts(col(4), r("pci", 3, 4), -STEP, ALU.mult, 3 * STEP, ALU.add)
-    ts(col(5), r("pci", 3, 4), -STEP, ALU.mult, 3 * STEP - 768.0, ALU.add)
-    ts(col(6), r("pci", 3, 4), -STEP, ALU.mult, 3 * STEP - 1520.0, ALU.add)
+    ts(col(6), r("pci", 1, 2), -STEP, ALU.mult, 15 * STEP - 64.0, ALU.add)
     cp(r("offu"), r("ramp", 0, 128, 16))
+    tt(col(5), col(6), col(2), ALU.add)
+    ts(r("a3"), r("modi", 0, A), col(1), ALU.is_gt, FAR + STEP, ALU.mult)
+    ts(r("a2"), r("mod4"), col(3), ALU.is_gt, FAR + STEP, ALU.mult)
     for t in range(R):
         act(r("lw%d" % t, C + 1, LW, 2), r("ramp", 0, A), ACT.Identity, scale=0.0, bias=EMPTY)
-        for a in range(4):
-            zero("h1p", a * PL + tsec(t) - 16, 16)
-        zero(gw[t], 0, 16)
-    zero("m0", 0, 16)
-    zero("g0", 0, 16)
+    for a in range(4):
+        zero("h1p", a * HP, 16)
+    for name in ("g1", "m0", "g0"):
+        zero(name, 0, 16)
     zero("fl", 0, 2)
+    act(r("lane"), r("ramp", 0, C, 16), ACT.Identity, bias=col(1))
     for i in range(2):
-        quant("s", half * i, half, r("gw0", 16 + 4 * half * i, 16 + 4 * half * (i + 1)))
-        send(r("qs", half * i, half * (i + 1)), r("ql", half * i, half * (i + 1)), "arr0", "sent0", True)
-    send(r("cs", 0, C), r("cl", 0, C), "arr0", "sent0", False)
-    arrives([r("ql", 0, C), r("cl", 0, C)], "arr0", 3)
-    quant("s", C, C, r("h2"))
-    send_pair(C, C, "arr1", "sent0")
+        act(r("src", 24 * i, 24 * i + 24), r("lane"), ACT.Copy)
+        act(r("jk", 24 * i, 24 * i + 24), r("lane"), ACT.Identity, bias=float(KS[i] - C))
+    act(r("val"), r("ramp"), ACT.Identity, scale=4.0, bias=col(2))
+    act(r("icat"), r("lane", 0, 16), ACT.Identity, bias=0.5)
+    act(r("tc"), r("lane", 0, 16), ACT.Identity, scale=4.0, bias=4.0 * (16 + C))
+    act(r("ramph"), r("ramp", 0, A), ACT.Identity, bias=0.5)
+    quant("s", C, C, r("h2w", 0, 4 * C))
+    send(r("cs", 0, 2 * C), r("cl", 0, 2 * C), "arr0", "sent0", False)
+    arrives([r("ql", 0, C), r("cl", 0, 2 * C)], "arr0", 1 + len(pieces))
+    send(r("qs", C, 2 * C), r("ql", C, 2 * C), "arr1", "sent0", True)
+    arrives([r("ql", C, 2 * C)], "arr1", 1)
     first_sent = ("sent0", total["sent0"])
     quant("e", 0, 512, r("et"))
-    planes("h1p", 0, h1(0), C, 0.5)
-    planes("h2p", 0, r("h2"), C)
+    act(r("a2"), r("a2"), ACT.Identity, bias=-FAR)
+    act(r("a3"), r("a3"), ACT.Identity, bias=-FAR)
+    planes("h1p", HP, 16, r("h1"), C, 0.5)
     quant("u", 0, 128, r("ub"))
     op("v", lambda: g.vector.tensor_copy(T.qup[:, 0:128].bitcast(dt.uint32),
                                          T.qu[:, 0:128].bitcast(dt.uint32).indirect(T.offu[:, 0:8])),
@@ -260,156 +295,178 @@ def rank_program(g, core, T, topo):
     quant("h0", 0, C, r("m0", 16))
     mm(2, "up", 0, "h0", 0, C)
     mm(3, "up", 0, "s", 0, C)
-    act(r("pe"), bank(2, C), ACT.Abs, scale=2.0 ** -24 + 2.0 ** -30)
-    act(r("pe"), r("pe"), ACT.Identity, bias=2.0 ** -122)
+    act(r("pe"), bank(2, C), ACT.Abs, scale=2.0 ** -24 + 2.0 ** -30, bias=2.0 ** -124)
     act(r("p1"), bank(3, C), ACT.Copy)
     dma("y", T.qw[:, 0:512].bitcast(dt.uint8), T.wc[:, 0:2048], [], [r("qw")], [first_sent])
     dma("y", T.cw[:, 0:512], T.ws[:, 0:512], [], [r("cw")])
     dma("y", ap(r("vb")), T.v[:], [], [r("vb")])
-    ts(r("modi"), r("rampi"), 15, ALU.bitwise_and)
-    ts(r("mod4"), r("rampi", 0, A), 3, ALU.bitwise_and)
     hold_pattern(0)
-    hold_pattern(1)
     tt(r("p0"), bank(2, C), r("pe"), ALU.add)
-    ts(r("a2"), r("mod4"), col(3), ALU.is_gt, 2.0 ** 20 + STEP, ALU.mult)
-    for i in range(2):
-        act(r("src", 24 * i, 24 * i + 24), r("ramp", 0, C, 16), ACT.Identity, bias=col(1))
-    for i in range(2):
-        act(r("jk", 24 * i, 24 * i + 24), r("src", 0, 24), ACT.Identity, bias=float(KS[i] - C))
-    act(r("val"), r("ramp"), ACT.Identity, scale=4.0, bias=col(2))
-    act(r("icat", 0, 60), r("ramp", 0, A, 4), ACT.Identity, bias=col(3))
-    act(r("icat", 60, 75), r("src", 0, 15), ACT.Identity, bias=0.5)
-    act(r("h2o", A + 3, 300, 4), r("src", 0, 15), ACT.Identity, bias=col(6))
-    act(r("ramph"), r("ramp", 0, A), ACT.Identity, bias=0.5)
-    act(r("a2"), r("a2"), ACT.Identity, bias=-2.0 ** 20)
 
-    s0, s1 = bank(4, C), bank(0, C)
-    for t in range(R):
-        m0, lw = ("g0" if t else "m0"), "lw%d" % t
-        ki = t % 2
+    runs, last = [(0, HS), (HS, C)], [(0, HF), (HF, C)]
 
-        for k in range(2):
-            b0 = 4 - 4 * k
-            if t == 0:
-                for b in range(4):
-                    mm(b0 + b, "e", 128 * b, "l", C * k, C)
-                if k:
-                    mm(4, "up", 0, "g0", 0, C)
-                for b in range(4):
-                    move("vs"[b % 2], log(k, 0, b), bank(b0 + b, C))
+    def step(word, t):
+        q, k, a = word[0], word[1], int(word[2:] or 0)
+        first, sec, at = t == 0, tsec(t - 1), 72 * (t - 1)
+        lo, hi = (runs if t < R else last)[a % 2]
+        sb = (1, 2) if first else (5, 6)
+        if k == "B":
+            lo, hi = ((0, CB), (CB, 60))[a]
+            move(q, r("zb", 16 * lo, 16 * hi), r("g1"), off=r("offz", lo, hi), scale=0.5)
+        elif k == "l":
+            n, arr = (24 if whole_out else 48), "arr%d" % (1 + t)
+            cp(r("srcu", at, at + 72), r("src"))
+            send(r("srcu", at, at + n), r("lland", 48 * (t - 1), 48 * (t - 1) + n), arr, "sent", False)
+            arrives([r("lland", 48 * (t - 1), 48 * t)], arr, 1)
+        elif k == "r":
+            relu(q, r("h1p", a * HP + 16 + C, (a + 1) * HP), 4 + a, 2.0 ** -6)
+        elif k == "z":
+            tt(r("z1", a, 4 * A, 4), r("h1p", a * HP, (a + 1) * HP), r("zb", a, 4 * A, 4), ALU.add,
+               off=r("offb", 0, 15))
+        elif k == "t":
+            relu(q, r("t0", a, 4 * A, 4), 4 + a, 2.0 ** -5)
+        elif k == "u":
+            quant("s", sent_t(t - 1, 0), A, r("t0"))
+            send_pair(sent_t(t - 1, 0), A, "arr%d" % (3 + t), land(t))
+        elif k == "W":
+            quant("z1", 0, A, r("z1"))
+            for b in range(4):
+                mm(b, "w", 128 * b, "z1", 0, A)
+        elif k == "R":
+            relu(q, r("h2w", 4 * sec + a, 4 * (sec + A), 4), a, 2.0 ** -5)
+        elif k == "T":
+            quant("s", sent_t(t - 1, 1), A, r("h2w", 4 * sec, 4 * (sec + A)))
+            send_pair(sent_t(t - 1, 1), A, "arr%d" % (5 + t), (sent_t(t - 1, 1), A))
+        elif k == "H":
+            move(q, r("h1", a, 4 * C, 4), r("h1p", a * HP, (a + 1) * HP), off=r("srcu", at + 48, at + 72), scale=2.0)
+        elif k == "h":
+            quant("s", sent_h1(t), C, r("h1"))
+            if whole_out:
+                send_pair(sent_h1(t), C, "arr%d" % (3 + t), land(t))
+        elif k == "P":
+            mm(7, "up", 0, "s", sent_h1(t), C)
+        elif k == "p":
+            move(q, r("p1"), bank(7, C))
+        elif k == "v":
+            if t == 1:
+                hold_pattern(1)
             else:
-                gp, lo = "gp%d" % k, tsec(t - 1)
-                for b in range(4):
-                    mm(b0 + b, "e", 128 * b, "l", tq(t - 1, k), A)
-                if k:
-                    mm(4, "up", 0, "g0", 0, C)
-                for b in range(4):
-                    move(("vsvs", "vsss")[k][b], r(gp, b * PL + lo, b * PL + lo + A), bank(b0 + b, A))
-                o = 48 * (t - 1) + 24 * (1 - k)
-                for a in range(4):
-                    move("vs"[a % 2], log(k, t, a), r(gp, a * PL, a * PL + lo + A), off=r("lland", o, o + 24))
-            if k or t == 0:
-                sum_in = h1(t) if k else r(m0, 16)
-                dma("g", ap(sum_in), ap(log(k, t)), [log(k, t)], [sum_in], accum_op=ALU.add)
-            quant("g%d" % k, 0, C, log(k, t))
-            if t and not k:
+                quant("v", 0, 128, r("vb"))
+        elif k == "D":
+            lo, n = (0, C) if first else land(t)
+            if a:
+                lo, n = (C + runs[a - 1][0], runs[a - 1][1] - runs[a - 1][0]) if first else (sent_t(t - 1, 1), A)
+            for b in range(4):
+                mm(((4, 5, 6, 7), (0, 1, 2, 3), (5, 6, 7, 0))[a][b], "e", 128 * b, "l", lo, n)
+        elif k == "C":
+            if first or whole_in:
+                move(q, log(0, t, a), bank(4 + a, C))
+            else:
+                move(q, r("gp0", a * PL + sec, a * PL + sec + A), bank(4 + a, A))
+        elif k == "G":
+            move(q, log(0, t, a), r("gp0", a * PL, a * PL + sec + A), off=r("lland", 48 * t - 24, 48 * t))
+        elif k == "Q":
+            if first:
+                dma("g", ap(r("m0", 16)), ap(log(0, 0)), [log(0, 0)], [r("m0", 16)], accum_op=ALU.add)
+            quant("g0", 0, C, log(0, t))
+            if not first:
                 dma("g", ap(log(0, t)), T.x[:, 0:4 * C], [], [log(0, t)], accum_op=ALU.add)
-        mm(0, "up", 0, "g1", 0, C)
-        if t == 0:
-            planes("gp0", 0, log(0, 0), C)
-        tt(r("mm"), s0, r("p1"), ALU.max)
-        tt(r("nn"), s1, r("p0"), ALU.max)
+        elif k == "S":
+            mm(4, "up", 0, "g0", 0, C)
+        elif k == "m":
+            tt(r("mm"), bank(4, C), r("p1"), ALU.max)
+        elif k == "n":
+            if not whole_in:
+                planes("gp0", PL, 0, log(0, 0), C)
+        elif k == "c":
+            if first:
+                lo, hi = runs[a // 4]
+                move(q, log(1, 0, a % 4, lo, hi), bank((0, 1, 2, 3, 5, 6, 7, 0)[a], hi - lo))
+            else:
+                move(q, r("gp1", a * PL + sec, a * PL + sec + A), bank(a, A))
+        elif k in "ab" and t < R:
+            lo, hi = runs[k == "b"]
+            move(q, log(1, t, a, lo, hi), r("gp1", a * PL, a * PL + sec + A),
+                 off=r("lland", 48 * (t - 1) + lo // 16, 48 * (t - 1) + hi // 16))
+        elif k == "q" and t < R:
+            quant("g1", lo, hi - lo, log(1, t, None, lo, hi))
+            mm(sb[a], "up", 0, "g1", lo, hi - lo)
+        elif k == "f":
+            s0, s1 = bank(4, hi - lo, lo), bank(sb[a], hi - lo)
+            tt(r("nn", lo, hi), s1, r("p0", lo, hi), ALU.max)
+            tt(r("fl", 2 + C + lo, 2 + C + hi), s1, r("mm", lo, hi), ALU.is_gt)
+            tt(r("fl", 2 + lo, 2 + hi), s0, r("nn", lo, hi), ALU.is_ge)
+        elif k == "L":
+            slots_out(R - 1)
+            wrote = dma("y", T.ol[:], T.ola[0:128:16, :], [r("ola")], [])
+            dma("g", T.ol[:], T.olb[0:128:16, :], [r("olb")], [], [wrote], accum_op=ALU.add)
+            for b in range(4):
+                ts(r("offf", 24 * b, 24 * b + 24), r("src", 0, 24), 4.0, ALU.mult, float(b), ALU.add)
+        elif k in "ab":
+            lo, hi = last[k == "b"]
+            move(q, r("h2f", 4 * lo + a, 4 * hi, 4), r("h2w"), off=r("offf", 24 * a + lo // 16, 24 * a + hi // 16))
+        elif k == "q":
+            quant("f", lo, hi - lo, r("h2f", 4 * lo, 4 * hi))
+            mm(4 + a, "v", 0, "f", lo, hi - lo)
+            dma("y", T.oc[:, 4 * lo:4 * hi], T.qf[:, lo:hi].bitcast(dt.uint8), [r("qf", lo, hi)], [])
+        elif k == "y":
+            move(q, r("yb", lo, hi), bank(4 + a, hi - lo))
+            dma("ys"[a], T.y[:, lo:hi], ap(r("yb", lo, hi)), [r("yb", lo, hi)], [])
+        elif k == "o":
+            dma(q, T.osc[4 * a:4 * a + 4, 0:C], T.cf[32 * a:32 * a + 4, 0:C], [r("cf")], [])
 
-        tt(r("fl", 2 + C, 2 + 2 * C), s1, r("mm"), ALU.is_gt)
-        tt(r("fl", 2, 2 + C), s0, r("nn"), ALU.is_ge)
+    for word in OPEN.split():
+        step(word, 0)
+    for t in range(R):
+        m0, lw, ki = ("g0" if t else "m0"), "lw%d" % t, t % 2
+
         act(r("junk"), r("fl", 2, 2 + C), ACT.Identity, scale=-1.0, acc=r("n0"))
-        act(r("sg", 0, 75), r("icat", 0, 75), ACT.Sign, bias=r("n0"))
-        act(r("xs", 0, 75), r("sg", 0, 75), ACT.Copy, scale=-768.0)
+        act(r("sg"), r("icat"), ACT.Sign, bias=r("n0"))
+        act(r("lev"), r("sg"), ACT.Identity, scale=-0.5, bias=0.5)
+        act(r("src", 48, 72), r("lane"), ACT.Identity, bias=16.0)
         act(r("sgo"), r("ramph"), ACT.Sign, bias=r("n0"))
         act(r("olb", A * t, A * t + A), r("sgo"), ACT.Copy, scale=192.0)
-        if t == 0:
-            planes("gp1", 0, log(1, 0), C)
-        else:
-            planes("h2p", tsec(t - 1), r("t1"), A)
         scan(r("cnt"), r("fl", 2, 2 + 2 * C), r("fl", 1, 1 + 2 * C), float(KS[t]), ALU.add, ALU.add)
         scan(r("held"), r("a1", 2 * C * ki, 2 * C * ki + 2 * C), r("cnt"), 0.0, ALU.max, ALU.min)
         cp(r("vi"), r("held", 15, 2 * C, 16))
         ts(r("par"), r("vi"), 1, ALU.bitwise_and)
         tt(r("yw", 24, 72), r("vi"), r("par"), ALU.mult)
+        tt(r("sg"), r("tc"), r("lev"), ALU.mult)
         tt(r("yw", 0, 24), r("yw", 24, 48), r("yw", 48, 72), ALU.max)
+        ts(r("cand", 48, 72), r("yw", 24, 48), 0.5, ALU.mult, 16 + C - 0.5 - KS[t] // 2, ALU.add)
         tt(r("ow"), r("yw", 0, 24), r("jk", 24 * ki, 24 * ki + 24), ALU.max)
+        ts(r("cand", 0, 48), r("yw", 0, 48), 0.5, ALU.mult, -0.5, ALU.add)
         ts(r("offs"), r("ow"), float(C - KS[t]), ALU.add)
+        act(r("e1"), r("sg"), ACT.Identity, bias=col(5))
+        if t == 0:
+            planes("gp1", PL, 0, log(1, 0), C)
+        else:
+            planes("h1p", HP, 16, r("h1"), C, 0.5)
+            slots_out(t - 1)
+        if t < R - 1:
+            tt(r("src"), r("src"), r("cand"), ALU.max)
+        else:
+            ts(r("cand2"), r("yw", 0, 24), 0.0, ALU.is_gt, float(2 * SEC), ALU.mult)
         op("v", lambda: g.vector.tensor_copy(ap(r(lw)).indirect(ap(r("offs"))), ap(r("val"))),
            [r("val"), r("offs")], [r(lw)])
-        scan(r("h2o", 0, A), r("a2"), r(lw, C + 1, LW, 2), 0.0, ALU.add, ALU.max)
-        ts(r("offz"), r("h2o", 3, A, 4), col(4), ALU.subtract, 0.0, ALU.max)
-        move("s", r("z0", 0, 16 * CZ), r(m0), off=r("offz", 0, CZ), scale=0.5)
-        tt(r("vb2", 0, 75), r("h2o", 3, 300, 4), r("xs", 0, 75), ALU.add)
-        move("v", r("z0", 16 * CZ), r(m0), off=r("offz", CZ, 60), scale=0.5)
-        ts(r("offb", 0, 75), r("vb2", 0, 75), col(5), ALU.subtract, 0.0, ALU.max)
+        if t < R - 1:
+            step("vl", t + 1)
+        else:
+            tt(r("cand", 0, 24), r("cand", 0, 24), r("cand2"), ALU.add)
+        scan(r("h4"), r("a2"), r(lw, C + 1, LW, 2), 0.0, ALU.add, ALU.max)
+        scan(r("h16"), r("a3"), r(lw, C + 1, LW, 2), 0.0, ALU.add, ALU.max)
+        ts(r("offz"), r("h4", 3, A, 4), col(4), ALU.subtract, 0.0, ALU.max)
+        tt(r("vb2", 0, 15), r("h16", 15, A, 16), r("e1", 0, 15), ALU.max)
 
+        move("s", r("z0", 0, 16 * CZ), r(m0), off=r("offz", 0, CZ), scale=0.5)
+        move("v", r("z0", 16 * CZ), r(m0), off=r("offz", CZ, 60), scale=0.5)
+        ts(r("offb", 0, 15), r("vb2", 0, 15), col(5), ALU.subtract, 0.25, ALU.mult)
+        if t == R - 1:
+            tt(r("src", 0, 24), r("src", 0, 24), r("cand", 0, 24), ALU.max)
         quant("z0", 0, A, r("z0"))
         for a in range(4):
             mm(4 + a, "w", 128 * a, "z0", 0, A)
-        bw = r(gw[t], 0, 16 + 8 * C)
-        move("s", r("zb", 0, 16 * CB), bw, off=r("offb", 0, CB), scale=0.5)
-        move("v", r("zb", 16 * CB), bw, off=r("offb", CB, 60), scale=0.5)
-        for a in range(4):
-            relu("s", r("h1p", a * PL + tsec(t), a * PL + tsec(t) + A), 4 + a, 2.0 ** -6)
-        for a in range(4):
-            tt(r("z1", a, 4 * A, 4), r("h1p", a * PL + tsec(t) - 16, a * PL + tsec(t) + A), r("zb", a, 4 * A, 4),
-               ALU.add, off=r("offb", 60, 75))
-        if t < 2:
-            for a in range(4):
-                relu("s", r("t0", a, 4 * A, 4), 4 + a, 2.0 ** -5)
-            quant("s", tq(t, 0), A, r("t0"))
-            send_pair(tq(t, 0), A, "arr%d" % (4 + t), "sent")
 
-        quant("z1", 0, A, r("z1"))
-        for a in range(4):
-            mm(a, "w", 128 * a, "z1", 0, A)
-        ts(r("cand"), r("yw", 0, 48), 0.5, ALU.mult, -0.5, ALU.add)
-        if t < 2:
-            tt(r("src"), r("src"), r("cand"), ALU.max)
-            mine, theirs, arr = r("srcu", 48 * t, 48 * t + 48), r("lland", 48 * t, 48 * t + 48), "arr%d" % (2 + t)
-            cp(mine, r("src"))
-            send(mine, theirs, arr, "sent", False)
-            arrives([theirs], arr, 1)
-        else:
-            ts(r("cand2"), r("yw", 0, 24), 0.0, ALU.is_gt, float(2 * SEC), ALU.mult)
-            act(r("ola", A * t, A * t + A), r(lw, C + 1, LW, 2), ACT.Identity, scale=0.25, bias=188.0)
-            wrote = dma("y", T.ol[:], T.ola[0:128:16, :], [r("ola")], [])
-            dma("g", T.ol[:], T.olb[0:128:16, :], [r("olb")], [], [wrote], accum_op=ALU.add)
-        for a in range(4):
-            made = r("t1", a, 4 * A, 4) if t < 2 else r("h2p", a * PL + tsec(t), a * PL + tsec(t) + A)
-            relu("vs"[a % 2], made, a, 2.0 ** -5)
-            if t == 2 and a == 0:
-                tt(r("cand", 0, 24), r("cand", 0, 24), r("cand2"), ALU.add)
-                tt(r("src", 0, 24), r("src", 0, 24), r("cand", 0, 24), ALU.max)
-                cp(r("offf"), r("src", 0, 24))
-        if t < 2:
-            quant("s", tq(t, 1), A, r("t1"))
-            send_pair(tq(t, 1), A, "arr%d" % (6 + t), "sent")
-            for a in range(4):
-                move("sv"[a % 2], r(gw[t + 1], 16 + a, 16 + 4 * C, 4), r("h1p", a * PL, a * PL + tsec(t) + A),
-                     off=r("srcu", 48 * t + 24, 48 * t + 48), scale=2.0)
-            if t == 0:
-                quant("v", 0, 128, r("vb"))
-            quant("h1", 0, C, h1(t + 1))
-            mm(3, "up", 0, "h1", 0, C)
-            act(r("ola", A * t, A * t + A), r(lw, C + 1, LW, 2), ACT.Identity, scale=0.25, bias=188.0)
-            act(r("p1"), bank(3, C), ACT.Copy)
-
-    for a in range(4):
-        move("vs"[a % 2], r("h2f", a, 4 * C, 4), r("h2p", a * PL, (a + 1) * PL), off=r("offf"))
-    quant("f", 0, C, r("h2f"))
-    mm(4, "v", 0, "f", 0, half)
-    mm(5, "v", 0, "f", half, half)
-    dma("y", T.oc[:, 0:4 * C], T.qf[:, 0:C].bitcast(dt.uint8), [r("qf")], [])
-    for k in range(4):
-        dma("yg"[k % 2], T.osc[4 * k:4 * k + 4, 0:C], T.cf[32 * k:32 * k + 4, 0:C], [r("cf")], [])
-    move("v", r("yb", 0, half), bank(4, half))
-    move("s", r("yb", half, C), bank(5, half))
-    dma("y", T.y[:, 0:half], ap(r("yb", 0, half)), [r("yb", 0, half)], [])
-    dma("s", T.y[:, half:C], ap(r("yb", half, C)), [r("yb", half, C)], [])
+        for word in ((RY if near_out else RX) if t < R - 1 else LAST + " " + END).split():
+            step(word, t + 1)
     wait("g", list(total.items()))

@@ -5,25 +5,30 @@ SEC = 256
 PL = C + R * SEC
 HP = 16 + C + A
 KS = [2 * (C + 16), 2 * (C + 16 + SEC), 2 * (C + 16)]
-LW = C + 2 * A
-EMPTY = -1524.0
-STEP, FAR = 4096.0, 2.0 ** 20
+LW = max(KS) + 2 * A
+MID = 191
+EMPTY = -576.0
+STEP, FAR = float(C), 8192.0
 BF, F32, I32, U16, F16 = "bfloat16", "float32", "int32", "uint16", "float16"
 CODE, PLANE = "float8_e4m3fn_x4", "uint8"
 NS = 4 * C + 4 * A
-CZ = 30
+CZ = 32
 CB = 34
 HS = 192
 HF = 192
 WHOLE = (False, True)
 
 P1 = 128
-OPEN = "tD0 tD1 vC0 sC1 vC2 sC3 vQ sc0 sc1 tD2 tS vc3 sc2 vq0 sc4 sc5 sc6 sc7 vm vq1 vf0 vf1 sn"
+PB = (3, 7)
+HR = 192
+EARLY = (3, 1)
+OPEN = "vv tD0 tD1 vC0 sC1 vC2 sC3 vQ sc0 sc1 tD2 tS vc3 sc2 vq0 sc4 sc5 sc6 sc7 vm vq1 vf0 vf1 sN sn"
 K0 = "sB0 vB1 sr0 vz0 sr1 vz1 sr2 vz2 sr3 vz3 "
-G1S = " sc0 sc1 va0 sc2 va1 sc3 sa2 va3 vq0 sb0 sb1 sb2 vb3 vm vq1 vf0 vf1"
-RX = K0 + "st0 st1 st2 st3 vu vW vR0 sR1 vR2 sR3 vT sH0 vH1 sH2 vH3 vh tP sp vv tD0 tD1 vC0 sC1 vC2 sC3 vQ tS" + G1S
-RY = K0 + "sH0 sH1 sH2 vW vH3 vh sR0 sR1 sR2 sR3 vT tP sp vv tD0 vC0 sC1 vC2 sC3 vG0 sG1 vG2 sG3 tD1 vQ tS" + G1S
-LAST = K0 + "vW vL"
+G1S = " sc0 sc1 va0 sc2 va1 sc3 sa2 va3 vq0 sb0 sb1 sb2 vb3 vm vq1 vf0 vf1 sE"
+SPL = True
+RX = K0 + "st0 st1 st2 st3 vW vu vR0 sR1 vR2 sR3 sH0 vT vH1 sH2 vH3 tJ0 sK0 sK1 vh sK2 sK3 tP tJ1 vU0 vp sK4 sK5 tD1 sK6 sK7 vv vU1 tS" + G1S
+RY = K0 + "sI0 sI1 sI2 sI3 vW vI7 vi0 sI4 sI5 vI6 vi1 sR0 sR1 vR2 sR3 vT tP sp vv tD0 vC0 sC1 vC2 sC3 vG0 sG1 vG2 sG3 tD1 vQ tS" + G1S
+LAST = K0 + "sL vW vF"
 END = "sR0 vR1 sR2 vR3 sa0 va1 sa2 va3 sb0 vq0 vb1 sb2 vb3 sy0 vq1 yo0 so1 yo2 so3 vy1"
 
 SCRATCH = {"acc": ("psum", [128, 4096], F32)}
@@ -38,17 +43,19 @@ for _n, _w in (("s", NS), ("l", NS), ("g0", C), ("g1", C), ("z0", A), ("z1", A),
                ("up", 128), ("v", 128), ("e", 512), ("w", 512), ("f", C)):
     _buf(CODE, **{"q" + _n: _w})
     _buf(PLANE, **{"c" + _n: _w})
-_buf(BF, h1=4 * C, g1=16 + 4 * C, m0=16 + 4 * C, g0=16 + 4 * C, g00=4 * C, h2w=4 * PL, h2f=4 * C)
+_buf(BF, h1=4 * C, g1=16 + 4 * C, m0=16 + 4 * C, g0=16 + 4 * C, g00=4 * C, h2=4 * C, h2p=4 * PL, h2f=4 * C, t1=4 * A)
+_buf(BF, lw0=LW, lw1=LW, lw2=LW, a2=A, a3=A, val=C)
+_buf(F16, h4=A)
 _buf(BF, gp0=4 * PL, gp1=4 * PL, h1p=4 * HP, t0=4 * A, z0=4 * A, z1=4 * A, zb=4 * A)
 _buf(BF, ub=512, vb=512, et=2048, fl=2 * C + 2, junk=C, modi=C, mod4=A)
-_buf(I32, pci=8, vi=48, par=48)
+_buf(I32, pci=8, even=48)
 _buf(F16, a1=4 * C, cnt=2 * C, held=2 * C)
-_buf(F32, lw0=LW, lw1=LW, lw2=LW, ramp=C, pcf=8, a2=A, a3=A, val=C, ramph=A, jk=48, pe=C, p0=C, p1=C, mm=C, nn=C)
-_buf(F32, yw=72, ow=24, h4=A, h16=A, n0=1, lane=24, icat=16, tc=16, sg=16, lev=16, e1=16, vb2=16, cand=72, cand2=24)
-_buf(F32, src=72, f4=96, sgo=A, ola=R * A, olb=R * A, yb=C)
-_buf(U16, offu=8, offs=24, offz=60, offb=16, srcu=144, lland=96, offf=96)
+_buf(F32, ramp=C, pcf=8, ramph=A, pair=96, keep=96, pe=C, p0=C, p1=C, mm=C, nn=C)
+_buf(F32, yw=96, ow=24, h16=A, n0=1, lane=24, icat=16, tc=16, sg=16, lev=16, e1=16, vb2=16, cand=72, cand2=24)
+_buf(F32, src=72, sgo=A, ola=R * A, olb=R * A, yb=C)
+_buf(U16, offu=8, offs=24, offz=60, offb=16, srcu=144, lland=96, offf=24)
 
-SEMAPHORES = (["nv", "ns", "nt", "ng", "sent0", "sent"] + ["arr%d" % i for i in range(8)]
+SEMAPHORES = (["nv", "ns", "nt", "ng", "sent0", "sent"] + ["arr%d" % i for i in range(11)]
               + ["d%d" % i for i in range(32)])
 
 
@@ -64,7 +71,7 @@ def rank_program(g, core, T, topo):
     near_out, near_in = topo.chip(core) == topo.chip(nxt), topo.chip(core) == topo.chip(prv)
     whole_out, whole_in = WHOLE[near_out], WHOLE[near_in]
     Q = {"v": g.vector, "s": g.scalar, "t": g.tensor, "g": g, "y": g.sync}
-    total, waited, seen, dmas = {}, {k: {} for k in Q}, {}, [0]
+    total, waited, seen, behind, dmas = {}, {k: {} for k in Q}, {}, {}, [0]
 
     def r(name, lo=0, hi=None, step=1):
         return (name, lo, SCRATCH[name][1][1] if hi is None else hi, step)
@@ -82,14 +89,17 @@ def rank_program(g, core, T, topo):
             return False
         return not (a[3] > 1 and a[3] == b[3] and a[1] % a[3] != b[1] % b[3])
 
-    def wait(q, toks):
+    def wait(q, toks, every=False):
         need = {}
         for s, n in toks:
             need[s] = max(need.get(s, 0), n)
         for s, n in need.items():
-            if waited[q].get(s, 0) < n:
+            vouched = any(behind.get((s2, n2), {}).get(s, 0) >= n for s2, n2 in need.items() if s2 != s)
+            if waited[q].get(s, 0) < n and (every or not vouched):
                 Q[q].wait_ge(T.sem[s], n)
-                waited[q][s] = n
+        for s, n in need.items():
+            for s2, n2 in list(behind.get((s, n), {}).items()) + [(s, n)]:
+                waited[q][s2] = max(waited[q].get(s2, 0), n2)
 
     def before(q, reads, writes, after):
         toks = list(after)
@@ -100,6 +110,7 @@ def rank_program(g, core, T, topo):
         wait(q, toks)
 
     def note(q, reads, writes, tok):
+        behind[tok] = dict(waited.get(q, {}))
         for x in reads:
             seen.setdefault(x[0], []).append((x, False, q, tok))
         for x in writes:
@@ -136,7 +147,8 @@ def rank_program(g, core, T, topo):
     def send_pair(lo, n, arr, land):
         send(r("qs", lo, lo + n), r("ql", lo, lo + n), arr, "sent", True)
         send(r("cs", lo, lo + n), r("cl", lo, lo + n), arr, "sent", False)
-        arrives([r("ql", land[0], sum(land)), r("cl", land[0], sum(land))], arr, 2)
+        if land:
+            arrives([r("ql", land[0], sum(land)), r("cl", land[0], sum(land))], arr, 2)
 
     def quant(name, lo, n, src):
         c, s = r("q" + name, lo, lo + n), r("c" + name, lo, lo + n)
@@ -220,49 +232,42 @@ def rank_program(g, core, T, topo):
         for a in range(4):
             act(r(name, a * width + lo, a * width + lo + n), r(src[0], src[1] + a, src[2], 4), ACT.Copy, scale=scale)
 
-    def hold_pattern(i):
-        for lo in (2 * C * i, 2 * C * i + C):
-            ts(r("a1", lo, lo + C), r("modi"), col(1), ALU.is_le, float(KS[i] + 2 * A), ALU.mult)
+    def hold_pattern(i, k):
+        lo = C * (2 * i + k)
+        ts(r("a1", lo, lo + C), r("modi"), col(1), ALU.is_le, float(KS[i] + 2 * A), ALU.mult)
 
     def zero(name, lo, n):
         act(r(name, lo, lo + n), r("ramp", 0, n), ACT.Copy, scale=0.0)
 
     def slots_out(t):
-        act(r("ola", A * t, A * t + A), r("lw%d" % t, C + 1, LW, 2), ACT.Identity, scale=0.25, bias=188.0)
+        act(r("ola", A * t, A * t + A), slots(t), ACT.Identity, bias=C // 2 + float(MID))
 
-    pieces = [(0, P1), (P1, C)] if P1 < C else [(0, C)]
+    def slots(t):
+        return r("lw%d" % t, KS[t] + 1, KS[t] + 2 * A, 2)
+
+    pieces = [(0, P1), (P1, C)]
     for lo, hi in pieces:
         dma("y", ap(r("h1", 4 * lo, 4 * hi)), T.x[:, 4 * (C + lo):4 * (C + hi)], [], [r("h1", 4 * lo, 4 * hi)])
-    dma("y", ap(r("h2w", 0, 4 * C)), T.x[:, 8 * C:12 * C], [], [r("h2w", 0, 4 * C)])
+    dma("y", ap(r("h2")), T.x[:, 8 * C:12 * C], [], [r("h2")])
     dma("y", ap(r("ub")), T.u[:], [], [r("ub")])
     dma("y", ap(r("m0", 16)), T.x[:, 0:4 * C], [], [r("m0", 16)])
 
     op("g", lambda: g.iota(ap(r("pci", 0, 1)), [[1, 1]], 0, 1), [], [r("pci", 0, 1)])
     iota(r("ramp"), [[1, C]])
     iota(r("modi"), [[0, C // 16], [1, 16]])
-    iota(r("mod4"), [[0, A // 4], [1, 4]])
     op("v", lambda: g.vector.memset(ap(r("et")), 0.0), [], [r("et")])
     cp(col(0), r("pci", 0, 1))
     ts(r("pci", 1, 2), r("pci", 0, 1), 15, ALU.bitwise_and)
     ts(r("pci", 2, 3), r("pci", 0, 1), 3, ALU.bitwise_and)
-    ts(r("pci", 3, 4), r("pci", 1, 2), 2, ALU.logical_shift_right)
+    cp(r("offu"), r("ramp", 0, 128, 16))
     cp(col(1), r("pci", 1, 2))
-    ts(col(2), r("pci", 2, 3), 16.0, ALU.add)
-    ts(col(3), r("pci", 3, 4), 0.5, ALU.add)
-    for lo, hi in pieces:
+    for i, (lo, hi) in enumerate(pieces):
         quant("s", lo, hi - lo, r("h1", 4 * lo, 4 * hi))
         send(r("qs", lo, hi), r("ql", lo, hi), "arr0", "sent0", True)
-        if lo == 0:
-            for b in range(4):
-                ts(r("et", 513 * b, 512 * b + 512, 4), r("ramp", 0, 128), col(0), ALU.is_equal)
-    ts(col(4), r("pci", 3, 4), -STEP, ALU.mult, 3 * STEP, ALU.add)
-    ts(col(6), r("pci", 1, 2), -STEP, ALU.mult, 15 * STEP - 64.0, ALU.add)
-    cp(r("offu"), r("ramp", 0, 128, 16))
-    tt(col(5), col(6), col(2), ALU.add)
-    ts(r("a3"), r("modi", 0, A), col(1), ALU.is_gt, FAR + STEP, ALU.mult)
-    ts(r("a2"), r("mod4"), col(3), ALU.is_gt, FAR + STEP, ALU.mult)
+        for b in range(2 * i, 2 * i + 2):
+            ts(r("et", 513 * b, 512 * b + 512, 4), r("ramp", 0, 128), col(0), ALU.is_equal)
     for t in range(R):
-        act(r("lw%d" % t, C + 1, LW, 2), r("ramp", 0, A), ACT.Identity, scale=0.0, bias=EMPTY)
+        act(slots(t), r("ramp", 0, A), ACT.Identity, scale=0.0, bias=EMPTY)
     for a in range(4):
         zero("h1p", a * HP, 16)
     for name in ("g1", "m0", "g0"):
@@ -271,39 +276,45 @@ def rank_program(g, core, T, topo):
     act(r("lane"), r("ramp", 0, C, 16), ACT.Identity, bias=col(1))
     for i in range(2):
         act(r("src", 24 * i, 24 * i + 24), r("lane"), ACT.Copy)
-        act(r("jk", 24 * i, 24 * i + 24), r("lane"), ACT.Identity, bias=float(KS[i] - C))
-    act(r("val"), r("ramp"), ACT.Identity, scale=4.0, bias=col(2))
+        act(r("pair", 48 * i + 1, 48 * i + 48, 2), r("lane"), ACT.Copy, scale=2.0 - 2 * i)
+    zero("keep", 0, 96)
+    act(r("val"), r("ramp"), ACT.Identity, bias=-float(MID))
     act(r("icat"), r("lane", 0, 16), ACT.Identity, bias=0.5)
-    act(r("tc"), r("lane", 0, 16), ACT.Identity, scale=4.0, bias=4.0 * (16 + C))
+    act(r("tc"), r("lane", 0, 16), ACT.Identity, bias=16.0 + C)
     act(r("ramph"), r("ramp", 0, A), ACT.Identity, bias=0.5)
-    quant("s", C, C, r("h2w", 0, 4 * C))
+    quant("s", C, C, r("h2"))
     send(r("cs", 0, 2 * C), r("cl", 0, 2 * C), "arr0", "sent0", False)
     arrives([r("ql", 0, C), r("cl", 0, 2 * C)], "arr0", 1 + len(pieces))
-    send(r("qs", C, 2 * C), r("ql", C, 2 * C), "arr1", "sent0", True)
-    arrives([r("ql", C, 2 * C)], "arr1", 1)
+    for arr, lo, hi in (("arr1", C, C + HS), ("arr10", C + HS, 2 * C)) if SPL else (("arr1", C, 2 * C),):
+        send(r("qs", lo, hi), r("ql", lo, hi), arr, "sent0", True)
+        arrives([r("ql", lo, hi)], arr, 1)
     first_sent = ("sent0", total["sent0"])
-    quant("e", 0, 512, r("et"))
-    act(r("a2"), r("a2"), ACT.Identity, bias=-FAR)
-    act(r("a3"), r("a3"), ACT.Identity, bias=-FAR)
-    planes("h1p", HP, 16, r("h1"), C, 0.5)
+    iota(r("mod4"), [[0, A // 4], [1, 4]])
     quant("u", 0, 128, r("ub"))
+    quant("e", 0, 512, r("et"))
     op("v", lambda: g.vector.tensor_copy(T.qup[:, 0:128].bitcast(dt.uint32),
                                          T.qu[:, 0:128].bitcast(dt.uint32).indirect(T.offu[:, 0:8])),
        [r("qu"), r("offu")], [r("qup")])
-    op("v", lambda: g.vector.tensor_copy(T.cup[:, 0:128], T.cu[:, 0:128].indirect(T.offu[:, 0:8])),
-       [r("cu"), r("offu")], [r("cup")])
+    move("s", r("cup"), r("cu"), off=r("offu"))
+    early = EARLY[near_in]
+    for a in range(early):
+        act(r("h1p", a * HP + 16, a * HP + 16 + C), r("h1", a, 4 * C, 4), ACT.Copy, scale=0.5)
     quant("h0", 0, C, r("m0", 16))
     mm(2, "up", 0, "h0", 0, C)
     mm(3, "up", 0, "s", 0, C)
+    ts(r("pci", 3, 4), r("pci", 1, 2), 2, ALU.logical_shift_right)
+    ts(col(2), r("pci", 2, 3), 4 * MID + 16 - 12 * STEP, ALU.add)
+    ts(col(5), r("pci", 1, 2), -STEP, ALU.mult, 15 * STEP - MID - 16, ALU.add)
+    ts(col(3), r("pci", 3, 4), 0.5, ALU.add)
+    ts(col(4), r("pci", 3, 4), 4 * STEP, ALU.mult, col(2), ALU.add)
     act(r("pe"), bank(2, C), ACT.Abs, scale=2.0 ** -24 + 2.0 ** -30, bias=2.0 ** -124)
     act(r("p1"), bank(3, C), ACT.Copy)
     dma("y", T.qw[:, 0:512].bitcast(dt.uint8), T.wc[:, 0:2048], [], [r("qw")], [first_sent])
     dma("y", T.cw[:, 0:512], T.ws[:, 0:512], [], [r("cw")])
     dma("y", ap(r("vb")), T.v[:], [], [r("vb")])
-    hold_pattern(0)
     tt(r("p0"), bank(2, C), r("pe"), ALU.add)
 
-    runs, last = [(0, HS), (HS, C)], [(0, HF), (HF, C)]
+    runs, last, hruns = [(0, HS), (HS, C)], [(0, HF), (HF, C)], [(0, HR), (HR, C)]
 
     def step(word, t):
         q, k, a = word[0], word[1], int(word[2:] or 0)
@@ -327,15 +338,24 @@ def rank_program(g, core, T, topo):
             relu(q, r("t0", a, 4 * A, 4), 4 + a, 2.0 ** -5)
         elif k == "u":
             quant("s", sent_t(t - 1, 0), A, r("t0"))
-            send_pair(sent_t(t - 1, 0), A, "arr%d" % (3 + t), land(t))
+            if HR and whole_in:
+                send_pair(sent_t(t - 1, 0), A, "arr%d" % (3 + t), (sent_h1(t), HR))
+                lo, hi = sent_h1(t) + HR, sent_h1(t) + C
+                arrives([r("ql", lo, hi), r("cl", lo, hi)], "arr%d" % (7 + t), 2)
+            else:
+                send_pair(sent_t(t - 1, 0), A, "arr%d" % (3 + t), land(t))
         elif k == "W":
             quant("z1", 0, A, r("z1"))
             for b in range(4):
                 mm(b, "w", 128 * b, "z1", 0, A)
         elif k == "R":
-            relu(q, r("h2w", 4 * sec + a, 4 * (sec + A), 4), a, 2.0 ** -5)
+            relu(q, r("t1", a, 4 * A, 4) if t < R else r("h2p", a * PL + sec, a * PL + sec + A), a, 2.0 ** -5)
+        elif k == "E":
+            planes("h2p", PL, sec, r("t1"), A)
+            for b in (2 * t - 2, 2 * t - 1):
+                act(r("h2p", b * PL, b * PL + C), r("h2", b, 4 * C, 4), ACT.Copy)
         elif k == "T":
-            quant("s", sent_t(t - 1, 1), A, r("h2w", 4 * sec, 4 * (sec + A)))
+            quant("s", sent_t(t - 1, 1), A, r("t1"))
             send_pair(sent_t(t - 1, 1), A, "arr%d" % (5 + t), (sent_t(t - 1, 1), A))
         elif k == "H":
             move(q, r("h1", a, 4 * C, 4), r("h1p", a * HP, (a + 1) * HP), off=r("srcu", at + 48, at + 72), scale=2.0)
@@ -343,15 +363,43 @@ def rank_program(g, core, T, topo):
             quant("s", sent_h1(t), C, r("h1"))
             if whole_out:
                 send_pair(sent_h1(t), C, "arr%d" % (3 + t), land(t))
+        elif k == "I":
+            lo, hi = hruns[a // 4]
+            move(q, r("h1", 4 * lo + a % 4, 4 * hi, 4), r("h1p", a % 4 * HP, (a % 4 + 1) * HP),
+                 off=r("srcu", at + 48 + lo // 16, at + 48 + hi // 16), scale=2.0)
+        elif k == "i":
+            lo, hi = hruns[a]
+            quant("s", sent_h1(t) + lo, hi - lo, r("h1", 4 * lo, 4 * hi))
+            send_pair(sent_h1(t) + lo, hi - lo, "arr%d" % (3 + t + 4 * a), None if a else land(t))
+        elif k == "J":
+            lo, hi = hruns[a]
+            for b in range(4):
+                mm(4 + b, "e", 128 * b, "l", sent_h1(t) + lo, hi - lo)
+        elif k == "K":
+            lo, hi = hruns[a // 4]
+            move(q, log(0, t, a % 4, lo, hi), bank(4 + a % 4, hi - lo))
+        elif k == "U":
+            lo, hi = hruns[a]
+            quant("g0", lo, hi - lo, log(0, t, None, lo, hi))
+            if a:
+                dma("g", ap(log(0, t)), T.x[:, 0:4 * C], [], [log(0, t)], accum_op=ALU.add)
         elif k == "P":
-            mm(7, "up", 0, "s", sent_h1(t), C)
+            mm(PB[near_out], "up", 0, "s", sent_h1(t), C)
         elif k == "p":
-            move(q, r("p1"), bank(7, C))
+            move(q, r("p1"), bank(PB[near_out], C))
         elif k == "v":
-            if t == 1:
-                hold_pattern(1)
+            if t < 2:
+                hold_pattern(t, 0)
+                hold_pattern(t, 1)
             else:
                 quant("v", 0, 128, r("vb"))
+        elif k == "w":
+            name, pattern, own = (("a2", r("mod4"), col(3)), ("a3", r("modi", 0, A), col(1)))[a]
+            ts(r(name), pattern, own, ALU.is_gt, FAR + STEP, ALU.mult)
+            act(r(name), r(name), ACT.Identity, bias=-FAR)
+        elif k == "N":
+            for a in range(early, 4):
+                act(r("h1p", a * HP + 16, a * HP + 16 + C), r("h1", a, 4 * C, 4), ACT.Copy, scale=0.5)
         elif k == "D":
             lo, n = (0, C) if first else land(t)
             if a:
@@ -397,14 +445,14 @@ def rank_program(g, core, T, topo):
             tt(r("fl", 2 + C + lo, 2 + C + hi), s1, r("mm", lo, hi), ALU.is_gt)
             tt(r("fl", 2 + lo, 2 + hi), s0, r("nn", lo, hi), ALU.is_ge)
         elif k == "L":
+            wrote = dma("y", T.ol[:], T.olb[0:128:16, :], [r("olb")], [])
             slots_out(R - 1)
-            wrote = dma("y", T.ol[:], T.ola[0:128:16, :], [r("ola")], [])
-            dma("g", T.ol[:], T.olb[0:128:16, :], [r("olb")], [], [wrote], accum_op=ALU.add)
-            for b in range(4):
-                ts(r("offf", 24 * b, 24 * b + 24), r("src", 0, 24), 4.0, ALU.mult, float(b), ALU.add)
+            dma("g", T.ol[:], T.ola[0:128:16, :], [r("ola")], [], [wrote], accum_op=ALU.add)
+        elif k == "F":
+            cp(r("offf"), r("src", 0, 24))
         elif k in "ab":
             lo, hi = last[k == "b"]
-            move(q, r("h2f", 4 * lo + a, 4 * hi, 4), r("h2w"), off=r("offf", 24 * a + lo // 16, 24 * a + hi // 16))
+            move(q, r("h2f", 4 * lo + a, 4 * hi, 4), r("h2p", a * PL, (a + 1) * PL), off=r("offf", lo // 16, hi // 16))
         elif k == "q":
             quant("f", lo, hi - lo, r("h2f", 4 * lo, 4 * hi))
             mm(4 + a, "v", 0, "f", lo, hi - lo)
@@ -427,46 +475,56 @@ def rank_program(g, core, T, topo):
         act(r("sgo"), r("ramph"), ACT.Sign, bias=r("n0"))
         act(r("olb", A * t, A * t + A), r("sgo"), ACT.Copy, scale=192.0)
         scan(r("cnt"), r("fl", 2, 2 + 2 * C), r("fl", 1, 1 + 2 * C), float(KS[t]), ALU.add, ALU.add)
+        if t == 0:
+            step("vw0", 0)
         scan(r("held"), r("a1", 2 * C * ki, 2 * C * ki + 2 * C), r("cnt"), 0.0, ALU.max, ALU.min)
-        cp(r("vi"), r("held", 15, 2 * C, 16))
-        ts(r("par"), r("vi"), 1, ALU.bitwise_and)
-        tt(r("yw", 24, 72), r("vi"), r("par"), ALU.mult)
+        if t == 0:
+            step("vw1", 0)
+        mine = r("held", 15, 2 * C, 16)
+        ts(r("even"), mine, 0.5, ALU.add)
+        cp(r("pair", 0, 96, 2), mine)
+        tt(r("keep", 1, 96, 2), mine, r("even"), ALU.is_lt)
+        scan(r("yw"), r("keep"), r("pair"), 0.0, ALU.mult, ALU.max)
+        tt(r("ow"), r("yw", 1, 48, 2), r("yw", 49, 96, 2), ALU.max)
+        cp(r("offs"), r("ow"))
         tt(r("sg"), r("tc"), r("lev"), ALU.mult)
-        tt(r("yw", 0, 24), r("yw", 24, 48), r("yw", 48, 72), ALU.max)
-        ts(r("cand", 48, 72), r("yw", 24, 48), 0.5, ALU.mult, 16 + C - 0.5 - KS[t] // 2, ALU.add)
-        tt(r("ow"), r("yw", 0, 24), r("jk", 24 * ki, 24 * ki + 24), ALU.max)
-        ts(r("cand", 0, 48), r("yw", 0, 48), 0.5, ALU.mult, -0.5, ALU.add)
-        ts(r("offs"), r("ow"), float(C - KS[t]), ALU.add)
+        if t:
+            slots_out(t - 1)
+        if t == R - 1:
+            act(r("cand2"), r("ow"), ACT.Sign, bias=-float(KS[t]))
+            act(r("cand2"), r("cand2"), ACT.Relu, scale=float(2 * SEC))
+        act(r("cand", 0, 24), r("ow"), ACT.Identity, scale=0.5, bias=-0.5)
+        if t < R - 1:
+            act(r("cand", 24, 48), r("yw", 1, 48, 2), ACT.Identity, scale=0.5, bias=-0.5)
+            act(r("cand", 48, 72), r("yw", 1, 48, 2), ACT.Identity, scale=0.5, bias=16 + C - 0.5 - KS[t] // 2)
         act(r("e1"), r("sg"), ACT.Identity, bias=col(5))
         if t == 0:
             planes("gp1", PL, 0, log(1, 0), C)
         else:
             planes("h1p", HP, 16, r("h1"), C, 0.5)
-            slots_out(t - 1)
-        if t < R - 1:
-            tt(r("src"), r("src"), r("cand"), ALU.max)
-        else:
-            ts(r("cand2"), r("yw", 0, 24), 0.0, ALU.is_gt, float(2 * SEC), ALU.mult)
         op("v", lambda: g.vector.tensor_copy(ap(r(lw)).indirect(ap(r("offs"))), ap(r("val"))),
            [r("val"), r("offs")], [r(lw)])
         if t < R - 1:
-            step("vl", t + 1)
+            tt(r("src"), r("src"), r("cand"), ALU.max)
         else:
             tt(r("cand", 0, 24), r("cand", 0, 24), r("cand2"), ALU.add)
-        scan(r("h4"), r("a2"), r(lw, C + 1, LW, 2), 0.0, ALU.add, ALU.max)
-        scan(r("h16"), r("a3"), r(lw, C + 1, LW, 2), 0.0, ALU.add, ALU.max)
-        ts(r("offz"), r("h4", 3, A, 4), col(4), ALU.subtract, 0.0, ALU.max)
-        tt(r("vb2", 0, 15), r("h16", 15, A, 16), r("e1", 0, 15), ALU.max)
+        scan(r("h4"), r("a2"), slots(t), 0.0, ALU.add, ALU.max)
+        if t < R - 1:
+            step("vl", t + 1)
+        else:
+            tt(r("src", 0, 24), r("src", 0, 24), r("cand", 0, 24), ALU.max)
+        ts(r("offz"), r("h4", 3, A, 4), 4.0, ALU.mult, col(4), ALU.add)
+        scan(r("h16"), r("a3"), slots(t), 0.0, ALU.add, ALU.max)
 
         move("s", r("z0", 0, 16 * CZ), r(m0), off=r("offz", 0, CZ), scale=0.5)
         move("v", r("z0", 16 * CZ), r(m0), off=r("offz", CZ, 60), scale=0.5)
-        ts(r("offb", 0, 15), r("vb2", 0, 15), col(5), ALU.subtract, 0.25, ALU.mult)
-        if t == R - 1:
-            tt(r("src", 0, 24), r("src", 0, 24), r("cand", 0, 24), ALU.max)
+        tt(r("vb2", 0, 15), r("h16", 15, A, 16), r("e1", 0, 15), ALU.max)
         quant("z0", 0, A, r("z0"))
+        ts(r("offb", 0, 15), r("vb2", 0, 15), col(5), ALU.subtract)
         for a in range(4):
             mm(4 + a, "w", 128 * a, "z0", 0, A)
 
         for word in ((RY if near_out else RX) if t < R - 1 else LAST + " " + END).split():
             step(word, t + 1)
-    wait("g", list(total.items()))
+    for s, n in total.items():
+        g.wait_ge(T.sem[s], n)

@@ -4,8 +4,8 @@ C, A, R = 384, 240, 3
 SEC = 256
 PL = C + R * SEC
 HP = 16 + C + A
-KS = [2 * (C + 16), 2 * (C + 16 + SEC), 2 * (C + 16)]
-LW = max(KS) + 2 * A
+K = 2 * (C + 16 + SEC)
+LW = K + 2 * A + 2
 MID = 191
 EMPTY = -576.0
 STEP, FAR = float(C), 8192.0
@@ -14,22 +14,24 @@ CODE, PLANE = "float8_e4m3fn_x4", "uint8"
 NS = 4 * C + 4 * A
 CZ = 32
 CB = 34
-HS = 192
-HF = 192
+HS = 224
+H0 = 256
+HF = 256
 WHOLE = (False, True)
 
 P1 = 128
 PB = (3, 7)
 HR = 192
-EARLY = (3, 1)
-OPEN = "vv tD0 tD1 vC0 sC1 vC2 sC3 vQ sc0 sc1 tD2 tS vc3 sc2 vq0 sc4 sc5 sc6 sc7 vm vq1 vf0 vf1 sN sn"
+EARLY = (1, 1)
+OPEN = "tD0 tD1 vC0 sC1 vC2 sC3 vv vQ sc0 sc1 tD2 tS vc3 sc2 vq0 sc4 sc5 sc6 sc7 vm vq1 vf0 vf1 sN sn"
 K0 = "sB0 vB1 sr0 vz0 sr1 vz1 sr2 vz2 sr3 vz3 "
-G1S = " sc0 sc1 va0 sc2 va1 sc3 sa2 va3 vq0 sb0 sb1 sb2 vb3 vm vq1 vf0 vf1 sE"
-SPL = True
-RX = K0 + "st0 st1 st2 st3 vW vu vR0 sR1 vR2 sR3 sH0 vT vH1 sH2 vH3 tJ0 sK0 sK1 vh sK2 sK3 tP tJ1 vU0 vp sK4 sK5 tD1 sK6 sK7 vv vU1 tS" + G1S
-RY = K0 + "sI0 sI1 sI2 sI3 vW vI7 vi0 sI4 sI5 vI6 vi1 sR0 sR1 vR2 sR3 vT tP sp vv tD0 vC0 sC1 vC2 sC3 vG0 sG1 vG2 sG3 tD1 vQ tS" + G1S
+G1S = " sc1 sc2 va0 sc3 va1 sa2 va3 sb0 vq0 sb1 vm sb2 sb3 vq1 vf0 vf1 sE gE"
+RX = (K0 + "st0 st1 st2 st3 vW vu vR0 sR1 vR2 sR3 sH0 vT vH1 sH2 vH3 tJ0 vh sK0 sK1 tP vK2 vK3 sp tJ1 vU0 "
+      "sK4 vK5 tD1 sK6 vK7 vc0 vU1 tS" + G1S)
+RY = (K0 + "sI0 sI1 sI2 sI3 vW vI7 vi0 gj0 sI4 sI5 vI6 vi1 gj1 sR0 sR1 vR2 sR3 vT tP sp tD0 vC0 sC1 vC2 sC3 "
+      "vG0 sG1 tD1 vG2 sG3 vc0 vQ tS" + G1S)
 LAST = K0 + "sL vW vF"
-END = "sR0 vR1 sR2 vR3 sa0 va1 sa2 va3 sb0 vq0 vb1 sb2 vb3 sy0 vq1 yo0 so1 yo2 so3 vy1"
+END = "sR0 vR1 sR2 vR3 sa0 va1 sa2 va3 sb0 vq0 sb1 vb3 sb2 vq1 sy0 yo0 so1 yo2 so3 vy1"
 
 SCRATCH = {"acc": ("psum", [128, 4096], F32)}
 
@@ -43,15 +45,15 @@ for _n, _w in (("s", NS), ("l", NS), ("g0", C), ("g1", C), ("z0", A), ("z1", A),
                ("up", 128), ("v", 128), ("e", 512), ("w", 512), ("f", C)):
     _buf(CODE, **{"q" + _n: _w})
     _buf(PLANE, **{"c" + _n: _w})
-_buf(BF, h1=4 * C, g1=16 + 4 * C, m0=16 + 4 * C, g0=16 + 4 * C, g00=4 * C, h2=4 * C, h2p=4 * PL, h2f=4 * C, t1=4 * A)
+_buf(BF, h1=4 * C, g1=16 + 4 * C, m0=16 + 4 * C, m1=16 + 4 * C, m2=16 + 4 * C, g0=4 * C, h2=4 * C, h2p=4 * PL, h2f=4 * C, t1=4 * A)
 _buf(BF, lw0=LW, lw1=LW, lw2=LW, a2=A, a3=A, val=C)
 _buf(F16, h4=A)
 _buf(BF, gp0=4 * PL, gp1=4 * PL, h1p=4 * HP, t0=4 * A, z0=4 * A, z1=4 * A, zb=4 * A)
-_buf(BF, ub=512, vb=512, et=2048, fl=2 * C + 2, junk=C, modi=C, mod4=A)
-_buf(I32, pci=8, even=48)
-_buf(F16, a1=4 * C, cnt=2 * C, held=2 * C)
-_buf(F32, ramp=C, pcf=8, ramph=A, pair=96, keep=96, pe=C, p0=C, p1=C, mm=C, nn=C)
-_buf(F32, yw=96, ow=24, h16=A, n0=1, lane=24, icat=16, tc=16, sg=16, lev=16, e1=16, vb2=16, cand=72, cand2=24)
+_buf(BF, ub=512, vb=512, et=2048, fl=2 * C + 4, junk=C, modi=C, mod4=A)
+_buf(I32, pci=8)
+_buf(F16, a1=2 * C, cnt=2 * C, held=2 * C, pair=96)
+_buf(F32, ramp=C, pcf=8, ramph=A, keep=96, pe=C, p0=C, p1=C, mm=C, nn=C)
+_buf(F32, yw=96, ow=24, h16=A, n0=1, v1=24, lane=24, icat=16, tc=16, sg=16, e1=16, vb2=16, cand=72, cand2=24)
 _buf(F32, src=72, sgo=A, ola=R * A, olb=R * A, yb=C)
 _buf(U16, offu=8, offs=24, offz=60, offb=16, srcu=144, lland=96, offf=24)
 
@@ -222,8 +224,12 @@ def rank_program(g, core, T, topo):
         return (sent_h1(t), C) if whole_in else (sent_t(t - 1, 0), A)
 
     def log(k, t, a=None, lo=0, hi=C):
-        name, base = ("g1", 16) if k else (("g0", 16) if t else ("g00", 0))
+        name, base = ("g1", 16) if k else ("g0", 0)
         return r(name, base + 4 * lo, base + 4 * hi) if a is None else r(name, base + 4 * lo + a, base + 4 * hi, 4)
+
+    def add_log(t, lo, hi):
+        into, part = r("m%d" % t, 16 + 4 * lo, 16 + 4 * hi), log(0, t, None, lo, hi)
+        dma("g", ap(into), ap(part), [part], [into], accum_op=ALU.add)
 
     def tsec(t):
         return C + 16 + SEC * t
@@ -232,9 +238,11 @@ def rank_program(g, core, T, topo):
         for a in range(4):
             act(r(name, a * width + lo, a * width + lo + n), r(src[0], src[1] + a, src[2], 4), ACT.Copy, scale=scale)
 
-    def hold_pattern(i, k):
-        lo = C * (2 * i + k)
-        ts(r("a1", lo, lo + C), r("modi"), col(1), ALU.is_le, float(KS[i] + 2 * A), ALU.mult)
+    def pool_copy(out, in_, n):
+        op("g", lambda: g.affine_select(ap(out), ap(in_), [[0, n]], ALU.is_gt, 0.0, 1, 0), [in_], [out])
+
+    def hold_pattern(i):
+        ts(r("a1", C * i, C * i + C), r("modi"), col(1), ALU.is_le, FAR if i else K + 2.0 * A, ALU.mult)
 
     def zero(name, lo, n):
         act(r(name, lo, lo + n), r("ramp", 0, n), ACT.Copy, scale=0.0)
@@ -243,7 +251,7 @@ def rank_program(g, core, T, topo):
         act(r("ola", A * t, A * t + A), slots(t), ACT.Identity, bias=C // 2 + float(MID))
 
     def slots(t):
-        return r("lw%d" % t, KS[t] + 1, KS[t] + 2 * A, 2)
+        return r("lw%d" % t, K + 2, LW, 2)
 
     pieces = [(0, P1), (P1, C)]
     for lo, hi in pieces:
@@ -270,22 +278,21 @@ def rank_program(g, core, T, topo):
         act(slots(t), r("ramp", 0, A), ACT.Identity, scale=0.0, bias=EMPTY)
     for a in range(4):
         zero("h1p", a * HP, 16)
-    for name in ("g1", "m0", "g0"):
+    for name in ("g1", "m0", "m1", "m2"):
         zero(name, 0, 16)
     zero("fl", 0, 2)
+    zero("fl", C + 2, 2)
     act(r("lane"), r("ramp", 0, C, 16), ACT.Identity, bias=col(1))
     for i in range(2):
         act(r("src", 24 * i, 24 * i + 24), r("lane"), ACT.Copy)
-        act(r("pair", 48 * i + 1, 48 * i + 48, 2), r("lane"), ACT.Copy, scale=2.0 - 2 * i)
     zero("keep", 0, 96)
     act(r("val"), r("ramp"), ACT.Identity, bias=-float(MID))
     act(r("icat"), r("lane", 0, 16), ACT.Identity, bias=0.5)
-    act(r("tc"), r("lane", 0, 16), ACT.Identity, bias=16.0 + C)
     act(r("ramph"), r("ramp", 0, A), ACT.Identity, bias=0.5)
     quant("s", C, C, r("h2"))
     send(r("cs", 0, 2 * C), r("cl", 0, 2 * C), "arr0", "sent0", False)
-    arrives([r("ql", 0, C), r("cl", 0, 2 * C)], "arr0", 1 + len(pieces))
-    for arr, lo, hi in (("arr1", C, C + HS), ("arr10", C + HS, 2 * C)) if SPL else (("arr1", C, 2 * C),):
+    arrives([r("ql", 0, C), r("cl", 0, 2 * C)], "arr0", 3)
+    for arr, lo, hi in (("arr1", C, C + H0), ("arr10", C + H0, 2 * C)):
         send(r("qs", lo, hi), r("ql", lo, hi), arr, "sent0", True)
         arrives([r("ql", lo, hi)], arr, 1)
     first_sent = ("sent0", total["sent0"])
@@ -307,6 +314,11 @@ def rank_program(g, core, T, topo):
     ts(col(5), r("pci", 1, 2), -STEP, ALU.mult, 15 * STEP - MID - 16, ALU.add)
     ts(col(3), r("pci", 3, 4), 0.5, ALU.add)
     ts(col(4), r("pci", 3, 4), 4 * STEP, ALU.mult, col(2), ALU.add)
+    ts(col(6), col(5), -1.0, ALU.mult, -16.0 - C, ALU.add)
+    for i in range(2):
+        ts(r("pair", 48 * i + 1, 48 * i + 48, 2), r("lane"), 2.0 - 2 * i, ALU.mult)
+    ts(r("tc"), r("lane", 0, 16), -1.0, ALU.mult, col(6), ALU.add)
+    hold_pattern(1)
     act(r("pe"), bank(2, C), ACT.Abs, scale=2.0 ** -24 + 2.0 ** -30, bias=2.0 ** -124)
     act(r("p1"), bank(3, C), ACT.Copy)
     dma("y", T.qw[:, 0:512].bitcast(dt.uint8), T.wc[:, 0:2048], [], [r("qw")], [first_sent])
@@ -314,16 +326,24 @@ def rank_program(g, core, T, topo):
     dma("y", ap(r("vb")), T.v[:], [], [r("vb")])
     tt(r("p0"), bank(2, C), r("pe"), ALU.add)
 
-    runs, last, hruns = [(0, HS), (HS, C)], [(0, HF), (HF, C)], [(0, HR), (HR, C)]
+    later, last, hruns = [(0, HS), (HS, C)], [(0, HF), (HF, C)], [(0, HR), (HR, C)]
 
     def step(word, t):
         q, k, a = word[0], word[1], int(word[2:] or 0)
         first, sec, at = t == 0, tsec(t - 1), 72 * (t - 1)
+        runs = [(0, H0), (H0, C)] if first else later
         lo, hi = (runs if t < R else last)[a % 2]
         sb = (1, 2) if first else (5, 6)
         if k == "B":
             lo, hi = ((0, CB), (CB, 60))[a]
             move(q, r("zb", 16 * lo, 16 * hi), r("g1"), off=r("offz", lo, hi), scale=0.5)
+        elif k == "x":
+            if a:
+                ts(r("offb", 0, 15), r("vb2", 0, 15), col(5), ALU.subtract)
+            else:
+                tt(r("vb2", 0, 15), r("h16", 15, A, 16), r("e1", 0, 15), ALU.max)
+        elif k == "k":
+            tt(r("src"), r("src"), r("cand"), ALU.max)
         elif k == "l":
             n, arr = (24 if whole_out else 48), "arr%d" % (1 + t)
             cp(r("srcu", at, at + 72), r("src"))
@@ -338,7 +358,7 @@ def rank_program(g, core, T, topo):
             relu(q, r("t0", a, 4 * A, 4), 4 + a, 2.0 ** -5)
         elif k == "u":
             quant("s", sent_t(t - 1, 0), A, r("t0"))
-            if HR and whole_in:
+            if whole_in:
                 send_pair(sent_t(t - 1, 0), A, "arr%d" % (3 + t), (sent_h1(t), HR))
                 lo, hi = sent_h1(t) + HR, sent_h1(t) + C
                 arrives([r("ql", lo, hi), r("cl", lo, hi)], "arr%d" % (7 + t), 2)
@@ -351,9 +371,11 @@ def rank_program(g, core, T, topo):
         elif k == "R":
             relu(q, r("t1", a, 4 * A, 4) if t < R else r("h2p", a * PL + sec, a * PL + sec + A), a, 2.0 ** -5)
         elif k == "E":
-            planes("h2p", PL, sec, r("t1"), A)
-            for b in (2 * t - 2, 2 * t - 1):
-                act(r("h2p", b * PL, b * PL + C), r("h2", b, 4 * C, 4), ACT.Copy)
+            if q == "s":
+                planes("h2p", PL, sec, r("t1"), A)
+            else:
+                for b in (2 * t - 2, 2 * t - 1):
+                    pool_copy(r("h2p", b * PL, b * PL + C), r("h2", b, 4 * C, 4), C)
         elif k == "T":
             quant("s", sent_t(t - 1, 1), A, r("t1"))
             send_pair(sent_t(t - 1, 1), A, "arr%d" % (5 + t), (sent_t(t - 1, 1), A))
@@ -361,8 +383,6 @@ def rank_program(g, core, T, topo):
             move(q, r("h1", a, 4 * C, 4), r("h1p", a * HP, (a + 1) * HP), off=r("srcu", at + 48, at + 72), scale=2.0)
         elif k == "h":
             quant("s", sent_h1(t), C, r("h1"))
-            if whole_out:
-                send_pair(sent_h1(t), C, "arr%d" % (3 + t), land(t))
         elif k == "I":
             lo, hi = hruns[a // 4]
             move(q, r("h1", 4 * lo + a % 4, 4 * hi, 4), r("h1p", a % 4 * HP, (a % 4 + 1) * HP),
@@ -370,7 +390,10 @@ def rank_program(g, core, T, topo):
         elif k == "i":
             lo, hi = hruns[a]
             quant("s", sent_h1(t) + lo, hi - lo, r("h1", 4 * lo, 4 * hi))
-            send_pair(sent_h1(t) + lo, hi - lo, "arr%d" % (3 + t + 4 * a), None if a else land(t))
+        elif k == "j":
+            lo, hi = hruns[a]
+            send_pair(sent_h1(t) + lo, hi - lo, "arr%d" % (3 + t + 4 * a),
+                      (sent_h1(t) + lo, hi - lo) if whole_in else None if a else land(t))
         elif k == "J":
             lo, hi = hruns[a]
             for b in range(4):
@@ -380,23 +403,17 @@ def rank_program(g, core, T, topo):
             move(q, log(0, t, a % 4, lo, hi), bank(4 + a % 4, hi - lo))
         elif k == "U":
             lo, hi = hruns[a]
+            add_log(t, lo, hi)
             quant("g0", lo, hi - lo, log(0, t, None, lo, hi))
-            if a:
-                dma("g", ap(log(0, t)), T.x[:, 0:4 * C], [], [log(0, t)], accum_op=ALU.add)
         elif k == "P":
             mm(PB[near_out], "up", 0, "s", sent_h1(t), C)
         elif k == "p":
             move(q, r("p1"), bank(PB[near_out], C))
         elif k == "v":
-            if t < 2:
-                hold_pattern(t, 0)
-                hold_pattern(t, 1)
-            else:
-                quant("v", 0, 128, r("vb"))
+            hold_pattern(0)
         elif k == "w":
             name, pattern, own = (("a2", r("mod4"), col(3)), ("a3", r("modi", 0, A), col(1)))[a]
             ts(r(name), pattern, own, ALU.is_gt, FAR + STEP, ALU.mult)
-            act(r(name), r(name), ACT.Identity, bias=-FAR)
         elif k == "N":
             for a in range(early, 4):
                 act(r("h1p", a * HP + 16, a * HP + 16 + C), r("h1", a, 4 * C, 4), ACT.Copy, scale=0.5)
@@ -414,18 +431,15 @@ def rank_program(g, core, T, topo):
         elif k == "G":
             move(q, log(0, t, a), r("gp0", a * PL, a * PL + sec + A), off=r("lland", 48 * t - 24, 48 * t))
         elif k == "Q":
-            if first:
-                dma("g", ap(r("m0", 16)), ap(log(0, 0)), [log(0, 0)], [r("m0", 16)], accum_op=ALU.add)
+            add_log(t, 0, C)
             quant("g0", 0, C, log(0, t))
-            if not first:
-                dma("g", ap(log(0, t)), T.x[:, 0:4 * C], [], [log(0, t)], accum_op=ALU.add)
         elif k == "S":
             mm(4, "up", 0, "g0", 0, C)
         elif k == "m":
             tt(r("mm"), bank(4, C), r("p1"), ALU.max)
         elif k == "n":
-            if not whole_in:
-                planes("gp0", PL, 0, log(0, 0), C)
+            for b in range(0 if whole_in else 4):
+                pool_copy(r("gp0", b * PL, b * PL + C), log(0, 0, b), C)
         elif k == "c":
             if first:
                 lo, hi = runs[a // 4]
@@ -442,7 +456,7 @@ def rank_program(g, core, T, topo):
         elif k == "f":
             s0, s1 = bank(4, hi - lo, lo), bank(sb[a], hi - lo)
             tt(r("nn", lo, hi), s1, r("p0", lo, hi), ALU.max)
-            tt(r("fl", 2 + C + lo, 2 + C + hi), s1, r("mm", lo, hi), ALU.is_gt)
+            tt(r("fl", 4 + C + lo, 4 + C + hi), s1, r("mm", lo, hi), ALU.is_gt)
             tt(r("fl", 2 + lo, 2 + hi), s0, r("nn", lo, hi), ALU.is_ge)
         elif k == "L":
             wrote = dma("y", T.ol[:], T.olb[0:128:16, :], [r("olb")], [])
@@ -466,38 +480,49 @@ def rank_program(g, core, T, topo):
     for word in OPEN.split():
         step(word, 0)
     for t in range(R):
-        m0, lw, ki = ("g0" if t else "m0"), "lw%d" % t, t % 2
+        m0, lw = "m%d" % t, "lw%d" % t
 
-        act(r("junk"), r("fl", 2, 2 + C), ACT.Identity, scale=-1.0, acc=r("n0"))
-        act(r("sg"), r("icat"), ACT.Sign, bias=r("n0"))
-        act(r("lev"), r("sg"), ACT.Identity, scale=-0.5, bias=0.5)
+        act(r("junk"), r("fl", 2, 2 + C), ACT.Identity, scale=-2.0, acc=r("n0"))
+        act(r("sg"), r("icat"), ACT.Sign, scale=2.0, bias=r("n0"))
         act(r("src", 48, 72), r("lane"), ACT.Identity, bias=16.0)
-        act(r("sgo"), r("ramph"), ACT.Sign, bias=r("n0"))
+        act(r("sgo"), r("ramph"), ACT.Sign, scale=2.0, bias=r("n0"))
         act(r("olb", A * t, A * t + A), r("sgo"), ACT.Copy, scale=192.0)
-        scan(r("cnt"), r("fl", 2, 2 + 2 * C), r("fl", 1, 1 + 2 * C), float(KS[t]), ALU.add, ALU.add)
+        for k in (1, 0):
+            lo = 2 + (C + 2) * k
+            scan(r("cnt", C * k, C * k + C), r("fl", lo, lo + C), r("fl", lo - 1, lo - 1 + C), float(K),
+                 ALU.add, ALU.add)
+        for k in (1, 0):
+            scan(r("held", C * k, C * k + C), r("a1", C * k, C * k + C), r("cnt", C * k, C * k + C), 0.0,
+                 ALU.max, ALU.min)
+        mine = [r("held", 15, C, 16), r("v1")]
+        ts(mine[1], r("held", C + 15, 2 * C, 16), r("n0"), ALU.subtract, K + 2.0 * A, ALU.min)
+        for k in range(2):
+            ts(r("pair", 48 * k, 48 * k + 48, 2), mine[k], 0.5, ALU.add)
+        for k in range(2):
+            tt(r("keep", 48 * k + 1, 48 * k + 48, 2), mine[k], r("pair", 48 * k, 48 * k + 48, 2), ALU.is_lt)
         if t == 0:
             step("vw0", 0)
-        scan(r("held"), r("a1", 2 * C * ki, 2 * C * ki + 2 * C), r("cnt"), 0.0, ALU.max, ALU.min)
+        if t == 1:
+            quant("v", 0, 128, r("vb"))
+        scan(r("yw"), r("keep"), r("pair"), 0.0, ALU.mult, ALU.max)
         if t == 0:
             step("vw1", 0)
-        mine = r("held", 15, 2 * C, 16)
-        ts(r("even"), mine, 0.5, ALU.add)
-        cp(r("pair", 0, 96, 2), mine)
-        tt(r("keep", 1, 96, 2), mine, r("even"), ALU.is_lt)
-        scan(r("yw"), r("keep"), r("pair"), 0.0, ALU.mult, ALU.max)
         tt(r("ow"), r("yw", 1, 48, 2), r("yw", 49, 96, 2), ALU.max)
         cp(r("offs"), r("ow"))
-        tt(r("sg"), r("tc"), r("lev"), ALU.mult)
+        tt(r("e1"), r("tc"), r("sg"), ALU.mult)
         if t:
             slots_out(t - 1)
+        else:
+            act(r("a2"), r("a2"), ACT.Identity, bias=-FAR)
+            act(r("a3"), r("a3"), ACT.Identity, bias=-FAR)
         if t == R - 1:
-            act(r("cand2"), r("ow"), ACT.Sign, bias=-float(KS[t]))
+            act(r("cand2"), r("ow"), ACT.Sign, bias=-float(K))
             act(r("cand2"), r("cand2"), ACT.Relu, scale=float(2 * SEC))
-        act(r("cand", 0, 24), r("ow"), ACT.Identity, scale=0.5, bias=-0.5)
+        at = tsec(t % 2) - 1.0 - K // 2
+        act(r("cand", 0, 24), r("ow"), ACT.Identity, scale=0.5, bias=at)
         if t < R - 1:
-            act(r("cand", 24, 48), r("yw", 1, 48, 2), ACT.Identity, scale=0.5, bias=-0.5)
-            act(r("cand", 48, 72), r("yw", 1, 48, 2), ACT.Identity, scale=0.5, bias=16 + C - 0.5 - KS[t] // 2)
-        act(r("e1"), r("sg"), ACT.Identity, bias=col(5))
+            act(r("cand", 24, 48), r("yw", 1, 48, 2), ACT.Identity, scale=0.5, bias=at)
+            act(r("cand", 48, 72), r("yw", 1, 48, 2), ACT.Identity, scale=0.5, bias=15.0 + C - K // 2)
         if t == 0:
             planes("gp1", PL, 0, log(1, 0), C)
         else:
@@ -505,7 +530,7 @@ def rank_program(g, core, T, topo):
         op("v", lambda: g.vector.tensor_copy(ap(r(lw)).indirect(ap(r("offs"))), ap(r("val"))),
            [r("val"), r("offs")], [r(lw)])
         if t < R - 1:
-            tt(r("src"), r("src"), r("cand"), ALU.max)
+            step("vk", t + 1)
         else:
             tt(r("cand", 0, 24), r("cand", 0, 24), r("cand2"), ALU.add)
         scan(r("h4"), r("a2"), slots(t), 0.0, ALU.add, ALU.max)
@@ -517,14 +542,21 @@ def rank_program(g, core, T, topo):
         scan(r("h16"), r("a3"), slots(t), 0.0, ALU.add, ALU.max)
 
         move("s", r("z0", 0, 16 * CZ), r(m0), off=r("offz", 0, CZ), scale=0.5)
-        move("v", r("z0", 16 * CZ), r(m0), off=r("offz", CZ, 60), scale=0.5)
-        tt(r("vb2", 0, 15), r("h16", 15, A, 16), r("e1", 0, 15), ALU.max)
+        began = move("v", r("z0", 16 * CZ), r(m0), off=r("offz", CZ, 60), scale=0.5)
+        if t < R - 1:
+            ahead = r("m%d" % (t + 1), 16)
+            dma("y", ap(ahead), T.x[:, 0:4 * C], [], [ahead], [began])
+        step("vx0", t + 1)
         quant("z0", 0, A, r("z0"))
-        ts(r("offb", 0, 15), r("vb2", 0, 15), col(5), ALU.subtract)
+        step("vx1", t + 1)
         for a in range(4):
             mm(4 + a, "w", 128 * a, "z0", 0, A)
 
+
         for word in ((RY if near_out else RX) if t < R - 1 else LAST + " " + END).split():
             step(word, t + 1)
-    for s, n in total.items():
-        g.wait_ge(T.sem[s], n)
+    stores = ["d%d" % i for i in range(dmas[0] - 8, dmas[0])]
+    late = ["nt", "ns", "nv"] + stores
+    for s in [s for s in total if s not in late] + late:
+        if waited["g"].get(s, 0) < total[s] or s in ("sent0", "sent") or s.startswith("arr"):
+            g.wait_ge(T.sem[s], total[s])

from concourse.mybir import dt, AluOpType as ALU, ActivationFunctionType as ACT

C, A, R = 384, 240, 3
SEC = 256
PL = C + R * SEC
HP = 16 + C + A
K = 2 * (C + 16 + SEC)
LW = K + 2 * A + 2
MID = 191
EMPTY = -576.0
STEP, FAR = float(C), 8192.0
BF, F32, I32, U16, F16 = "bfloat16", "float32", "int32", "uint16", "float16"
CODE, PLANE = "float8_e4m3fn_x4", "uint8"
NS = 4 * C + 4 * A
CZ = 32
CB = 34
HS = 224
H0 = 256
HF = 256
WHOLE = (False, True)

P1 = 128
PB = (3, 7)
HR = 192
EARLY = (1, 1)
OPEN = "tD0 tD1 vC0 sC1 vC2 sC3 vv vQ sc0 sc1 tD2 tS vc3 sc2 vq0 sc4 sc5 sc6 sc7 vm vq1 vf0 vf1 sN sn"
K0 = "sB0 vB1 sr0 vz0 sr1 vz1 sr2 vz2 sr3 vz3 "
G1S = " sc1 sc2 va0 sc3 va1 sa2 va3 sb0 vq0 sb1 vm sb2 sb3 vq1 vf0 vf1 sE gE"
RX = (K0 + "st0 st1 st2 st3 vW vu vR0 sR1 vR2 sR3 sH0 vT vH1 sH2 vH3 tJ0 vh sK0 sK1 tP vK2 vK3 sp tJ1 vU0 "
      "sK4 vK5 tD1 sK6 vK7 vc0 vU1 tS" + G1S)
RY = (K0 + "sI0 sI1 sI2 sI3 vW vI7 vi0 gj0 sI4 sI5 vI6 vi1 gj1 sR0 sR1 vR2 sR3 vT tP sp tD0 vC0 sC1 vC2 sC3 "
      "vG0 sG1 tD1 vG2 sG3 vc0 vQ tS" + G1S)
LAST = K0 + "sL vW vF"
END = "sR0 vR1 sR2 vR3 sa0 va1 sa2 va3 sb0 vq0 sb1 vb3 sb2 vq1 sy0 yo0 so1 yo2 so3 vy1"

SCRATCH = {"acc": ("psum", [128, 4096], F32)}


def _buf(dtype, **sizes):
    for name, n in sizes.items():
        SCRATCH[name] = ("sbuf", [128, n], dtype)


for _n, _w in (("s", NS), ("l", NS), ("g0", C), ("g1", C), ("z0", A), ("z1", A), ("h0", C), ("u", 128),
               ("up", 128), ("v", 128), ("e", 512), ("w", 512), ("f", C)):
    _buf(CODE, **{"q" + _n: _w})
    _buf(PLANE, **{"c" + _n: _w})
_buf(BF, h1=4 * C, g1=16 + 4 * C, m0=16 + 4 * C, m1=16 + 4 * C, m2=16 + 4 * C, g0=4 * C, h2=4 * C, h2p=4 * PL, h2f=4 * C, t1=4 * A)
_buf(BF, lw0=LW, lw1=LW, lw2=LW, a2=A, a3=A, val=C)
_buf(F16, h4=A)
_buf(BF, gp0=4 * PL, gp1=4 * PL, h1p=4 * HP, t0=4 * A, z0=4 * A, z1=4 * A, zb=4 * A)
_buf(BF, ub=512, vb=512, et=2048, fl=2 * C + 4, junk=C, modi=C, mod4=A)
_buf(I32, pci=8)
_buf(F16, a1=2 * C, cnt=2 * C, held=2 * C, pair=96)
_buf(F32, ramp=C, pcf=8, ramph=A, keep=96, pe=C, p0=C, p1=C, mm=C, nn=C)
_buf(F32, yw=96, ow=24, h16=A, n0=1, v1=24, lane=24, icat=16, tc=16, sg=16, e1=16, vb2=16, cand=72, cand2=24)
_buf(F32, src=72, sgo=A, ola=R * A, olb=R * A, yb=C)
_buf(U16, offu=8, offs=24, offz=60, offb=16, srcu=144, lland=96, offf=24)

SEMAPHORES = (["nv", "ns", "nt", "ng", "sent0", "sent"] + ["arr%d" % i for i in range(11)]
              + ["d%d" % i for i in range(32)])


def rank_program(g, core, T, topo):
    rank = T.rank_of(core)
    if rank is None:
        return
    cores = T.cores
    nxt, prv = cores[(rank + 1) % len(cores)], cores[(rank - 1) % len(cores)]
    rid, pid = topo.addr(nxt)[:2]
    mask = topo.mask(core, nxt)
    n_out, n_in = len(topo.engines(core, nxt)), len(topo.engines(prv, core))
    near_out, near_in = topo.chip(core) == topo.chip(nxt), topo.chip(core) == topo.chip(prv)
    whole_out, whole_in = WHOLE[near_out], WHOLE[near_in]
    Q = {"v": g.vector, "s": g.scalar, "t": g.tensor, "g": g, "y": g.sync}
    total, waited, seen, behind, dmas = {}, {k: {} for k in Q}, {}, {}, [0]

    def r(name, lo=0, hi=None, step=1):
        return (name, lo, SCRATCH[name][1][1] if hi is None else hi, step)

    def ap(x):
        return T[x[0]][:, x[1]:x[2]:x[3]] if x[3] > 1 else T[x[0]][:, x[1]:x[2]]

    def bank(b, n, lo=0):
        return ("acc", 512 * b + lo, 512 * b + lo + n, 1)

    def meet(a, b):
        if a[0] == "acc":
            return a[1] // 512 == b[1] // 512
        if a[2] <= b[1] or b[2] <= a[1]:
            return False
        return not (a[3] > 1 and a[3] == b[3] and a[1] % a[3] != b[1] % b[3])

    def wait(q, toks, every=False):
        need = {}
        for s, n in toks:
            need[s] = max(need.get(s, 0), n)
        for s, n in need.items():
            vouched = any(behind.get((s2, n2), {}).get(s, 0) >= n for s2, n2 in need.items() if s2 != s)
            if waited[q].get(s, 0) < n and (every or not vouched):
                Q[q].wait_ge(T.sem[s], n)
        for s, n in need.items():
            for s2, n2 in list(behind.get((s, n), {}).items()) + [(s, n)]:
                waited[q][s2] = max(waited[q].get(s2, 0), n2)

    def before(q, reads, writes, after):
        toks = list(after)
        for x, wr in [(x, False) for x in reads] + [(x, True) for x in writes]:
            for y, ywr, yq, tok in seen.get(x[0], []):
                if meet(x, y) and (wr or ywr or (x[0] == "acc" and yq != q)):
                    toks.append(tok)
        wait(q, toks)

    def note(q, reads, writes, tok):
        behind[tok] = dict(waited.get(q, {}))
        for x in reads:
            seen.setdefault(x[0], []).append((x, False, q, tok))
        for x in writes:
            seen.setdefault(x[0], []).append((x, True, q, tok))
        return tok

    def op(q, call, reads, writes, after=()):
        before(q, reads, writes, after)
        s = "n" + q
        call().then_inc(T.sem[s], 1)
        total[s] = total.get(s, 0) + 1
        return note(q, reads, writes, (s, total[s]))

    def dma(q, out, in_, reads, writes, after=(), **kw):
        before(q, reads, writes, after)
        s = "d%d" % dmas[0]
        dmas[0] += 1
        Q[q].dma_start(out, in_, **kw).then_inc(T.sem[s], 16)
        total[s] = 16
        return note(q, reads, writes, (s, 16))

    def send(src, dst, arr, local, bits):
        before("g", [src], [], ())
        a, b = ap(src), ap(dst)
        if bits:
            a, b = a.bitcast(dt.uint8), b.bitcast(dt.uint8)
        g.remote_dma(b, a, T.sem[arr], T.sem[local], pid, rid, mask)
        total[local] = total.get(local, 0) + n_out

    def arrives(regions, arr, calls):
        total[arr] = calls * n_in
        note("x", [], regions, (arr, calls * n_in))

    def send_pair(lo, n, arr, land):
        send(r("qs", lo, lo + n), r("ql", lo, lo + n), arr, "sent", True)
        send(r("cs", lo, lo + n), r("cl", lo, lo + n), arr, "sent", False)
        if land:
            arrives([r("ql", land[0], sum(land)), r("cl", land[0], sum(land))], arr, 2)

    def quant(name, lo, n, src):
        c, s = r("q" + name, lo, lo + n), r("c" + name, lo, lo + n)
        return op("v", lambda: g.vector.quantize_mx(ap(c), ap(s), ap(src)), [src], [c, s])

    def mm(b, wn, wlo, xn, xlo, n):
        wc, ws = r("q" + wn, wlo, wlo + 128), r("c" + wn, wlo, wlo + 128)
        xc, xs = r("q" + xn, xlo, xlo + n), r("c" + xn, xlo, xlo + n)
        o = bank(b, n)
        return op("t", lambda: g.tensor.matmul_mx(ap(o), ap(wc), ap(ws), ap(xc), ap(xs), True, True),
                  [wc, ws, xc, xs], [o])

    def src_ap(x, off):
        return ap(x) if off is None else ap(x).indirect(ap(off))

    def ts(out, in0, s1, op0, s2=None, op1=None, off=None):
        reads = [in0] + [s for s in (s1, s2, off) if isinstance(s, tuple)]
        a1 = ap(s1) if isinstance(s1, tuple) else s1
        a2 = ap(s2) if isinstance(s2, tuple) else s2
        if op1 is None:
            return op("v", lambda: g.vector.tensor_scalar(ap(out), src_ap(in0, off), a1, None, op0), reads, [out])
        return op("v", lambda: g.vector.tensor_scalar(ap(out), src_ap(in0, off), a1, a2, op0, op1), reads, [out])

    def tt(out, in0, in1, o, off=None):
        return op("v", lambda: g.vector.tensor_tensor(ap(out), src_ap(in0, off), ap(in1), o),
                  [in0, in1] + ([off] if off else []), [out])

    def cp(out, in_, off=None):
        return op("v", lambda: g.vector.tensor_copy(ap(out), src_ap(in_, off)), [in_] + ([off] if off else []), [out])

    def scan(out, d0, d1, init, op0, op1):
        return op("v", lambda: g.vector.tensor_tensor_scan(ap(out), ap(d0), ap(d1), init, op0, op1), [d0, d1], [out])

    def act(out, in_, func, scale=None, bias=None, off=None, acc=None):
        kw = {}
        if scale is not None:
            kw["scale"] = scale
        if bias is not None:
            kw["bias"] = ap(bias) if isinstance(bias, tuple) else bias
        if acc is not None:
            kw["accum_out"] = ap(acc)
        reads = [in_] + [s for s in (bias, off) if isinstance(s, tuple)]
        return op("s", lambda: g.scalar.activation(ap(out), src_ap(in_, off), func, **kw), reads,
                  [out] + ([acc] if acc else []))

    def move(q, out, in_, off=None, scale=None):
        if q == "s":
            return act(out, in_, ACT.Copy, scale=scale, off=off)
        if scale is None:
            return cp(out, in_, off)
        return ts(out, in_, scale, ALU.mult, off=off)

    def relu(q, out, b, scale):
        if q == "s":
            return act(out, bank(b, A), ACT.Relu, scale=scale)
        return ts(out, bank(b, A), 0.0, ALU.max, scale, ALU.mult)

    def iota(out, pattern):
        op("g", lambda: g.iota(ap(out), pattern, 0, 0, allow_small_or_imprecise_dtypes=True), [], [out])

    def col(i):
        return r("pcf", i, i + 1)

    def sent_h1(t):
        return 2 * C + (C + A) * (t - 1) if t else 0

    def sent_t(t, k):
        return 3 * C + (C + A) * t if k else 4 * C + 2 * A + A * t

    def land(t):
        return (sent_h1(t), C) if whole_in else (sent_t(t - 1, 0), A)

    def log(k, t, a=None, lo=0, hi=C):
        name, base = ("g1", 16) if k else ("g0", 0)
        return r(name, base + 4 * lo, base + 4 * hi) if a is None else r(name, base + 4 * lo + a, base + 4 * hi, 4)

    def add_log(t, lo, hi):
        into, part = r("m%d" % t, 16 + 4 * lo, 16 + 4 * hi), log(0, t, None, lo, hi)
        dma("g", ap(into), ap(part), [part], [into], accum_op=ALU.add)

    def tsec(t):
        return C + 16 + SEC * t

    def planes(name, width, lo, src, n, scale=None):
        for a in range(4):
            act(r(name, a * width + lo, a * width + lo + n), r(src[0], src[1] + a, src[2], 4), ACT.Copy, scale=scale)

    def pool_copy(out, in_, n):
        op("g", lambda: g.affine_select(ap(out), ap(in_), [[0, n]], ALU.is_gt, 0.0, 1, 0), [in_], [out])

    def hold_pattern(i):
        ts(r("a1", C * i, C * i + C), r("modi"), col(1), ALU.is_le, FAR if i else K + 2.0 * A, ALU.mult)

    def zero(name, lo, n):
        act(r(name, lo, lo + n), r("ramp", 0, n), ACT.Copy, scale=0.0)

    def slots_out(t):
        act(r("ola", A * t, A * t + A), slots(t), ACT.Identity, bias=C // 2 + float(MID))

    def slots(t):
        return r("lw%d" % t, K + 2, LW, 2)

    pieces = [(0, P1), (P1, C)]
    for lo, hi in pieces:
        dma("y", ap(r("h1", 4 * lo, 4 * hi)), T.x[:, 4 * (C + lo):4 * (C + hi)], [], [r("h1", 4 * lo, 4 * hi)])
    dma("y", ap(r("h2")), T.x[:, 8 * C:12 * C], [], [r("h2")])
    dma("y", ap(r("ub")), T.u[:], [], [r("ub")])
    dma("y", ap(r("m0", 16)), T.x[:, 0:4 * C], [], [r("m0", 16)])

    op("g", lambda: g.iota(ap(r("pci", 0, 1)), [[1, 1]], 0, 1), [], [r("pci", 0, 1)])
    iota(r("ramp"), [[1, C]])
    iota(r("modi"), [[0, C // 16], [1, 16]])
    op("v", lambda: g.vector.memset(ap(r("et")), 0.0), [], [r("et")])
    cp(col(0), r("pci", 0, 1))
    ts(r("pci", 1, 2), r("pci", 0, 1), 15, ALU.bitwise_and)
    ts(r("pci", 2, 3), r("pci", 0, 1), 3, ALU.bitwise_and)
    cp(r("offu"), r("ramp", 0, 128, 16))
    cp(col(1), r("pci", 1, 2))
    for i, (lo, hi) in enumerate(pieces):
        quant("s", lo, hi - lo, r("h1", 4 * lo, 4 * hi))
        send(r("qs", lo, hi), r("ql", lo, hi), "arr0", "sent0", True)
        for b in range(2 * i, 2 * i + 2):
            ts(r("et", 513 * b, 512 * b + 512, 4), r("ramp", 0, 128), col(0), ALU.is_equal)
    for t in range(R):
        act(slots(t), r("ramp", 0, A), ACT.Identity, scale=0.0, bias=EMPTY)
    for a in range(4):
        zero("h1p", a * HP, 16)
    for name in ("g1", "m0", "m1", "m2"):
        zero(name, 0, 16)
    zero("fl", 0, 2)
    zero("fl", C + 2, 2)
    act(r("lane"), r("ramp", 0, C, 16), ACT.Identity, bias=col(1))
    for i in range(2):
        act(r("src", 24 * i, 24 * i + 24), r("lane"), ACT.Copy)
    zero("keep", 0, 96)
    act(r("val"), r("ramp"), ACT.Identity, bias=-float(MID))
    act(r("icat"), r("lane", 0, 16), ACT.Identity, bias=0.5)
    act(r("ramph"), r("ramp", 0, A), ACT.Identity, bias=0.5)
    quant("s", C, C, r("h2"))
    send(r("cs", 0, 2 * C), r("cl", 0, 2 * C), "arr0", "sent0", False)
    arrives([r("ql", 0, C), r("cl", 0, 2 * C)], "arr0", 3)
    for arr, lo, hi in (("arr1", C, C + H0), ("arr10", C + H0, 2 * C)):
        send(r("qs", lo, hi), r("ql", lo, hi), arr, "sent0", True)
        arrives([r("ql", lo, hi)], arr, 1)
    first_sent = ("sent0", total["sent0"])
    iota(r("mod4"), [[0, A // 4], [1, 4]])
    quant("u", 0, 128, r("ub"))
    quant("e", 0, 512, r("et"))
    op("v", lambda: g.vector.tensor_copy(T.qup[:, 0:128].bitcast(dt.uint32),
                                         T.qu[:, 0:128].bitcast(dt.uint32).indirect(T.offu[:, 0:8])),
       [r("qu"), r("offu")], [r("qup")])
    move("s", r("cup"), r("cu"), off=r("offu"))
    early = EARLY[near_in]
    for a in range(early):
        act(r("h1p", a * HP + 16, a * HP + 16 + C), r("h1", a, 4 * C, 4), ACT.Copy, scale=0.5)
    quant("h0", 0, C, r("m0", 16))
    mm(2, "up", 0, "h0", 0, C)
    mm(3, "up", 0, "s", 0, C)
    ts(r("pci", 3, 4), r("pci", 1, 2), 2, ALU.logical_shift_right)
    ts(col(2), r("pci", 2, 3), 4 * MID + 16 - 12 * STEP, ALU.add)
    ts(col(5), r("pci", 1, 2), -STEP, ALU.mult, 15 * STEP - MID - 16, ALU.add)
    ts(col(3), r("pci", 3, 4), 0.5, ALU.add)
    ts(col(4), r("pci", 3, 4), 4 * STEP, ALU.mult, col(2), ALU.add)
    ts(col(6), col(5), -1.0, ALU.mult, -16.0 - C, ALU.add)
    for i in range(2):
        ts(r("pair", 48 * i + 1, 48 * i + 48, 2), r("lane"), 2.0 - 2 * i, ALU.mult)
    ts(r("tc"), r("lane", 0, 16), -1.0, ALU.mult, col(6), ALU.add)
    hold_pattern(1)
    act(r("pe"), bank(2, C), ACT.Abs, scale=2.0 ** -24 + 2.0 ** -30, bias=2.0 ** -124)
    act(r("p1"), bank(3, C), ACT.Copy)
    dma("y", T.qw[:, 0:512].bitcast(dt.uint8), T.wc[:, 0:2048], [], [r("qw")], [first_sent])
    dma("y", T.cw[:, 0:512], T.ws[:, 0:512], [], [r("cw")])
    dma("y", ap(r("vb")), T.v[:], [], [r("vb")])
    tt(r("p0"), bank(2, C), r("pe"), ALU.add)

    later, last, hruns = [(0, HS), (HS, C)], [(0, HF), (HF, C)], [(0, HR), (HR, C)]

    def step(word, t):
        q, k, a = word[0], word[1], int(word[2:] or 0)
        first, sec, at = t == 0, tsec(t - 1), 72 * (t - 1)
        runs = [(0, H0), (H0, C)] if first else later
        lo, hi = (runs if t < R else last)[a % 2]
        sb = (1, 2) if first else (5, 6)
        if k == "B":
            lo, hi = ((0, CB), (CB, 60))[a]
            move(q, r("zb", 16 * lo, 16 * hi), r("g1"), off=r("offz", lo, hi), scale=0.5)
        elif k == "x":
            if a:
                ts(r("offb", 0, 15), r("vb2", 0, 15), col(5), ALU.subtract)
            else:
                tt(r("vb2", 0, 15), r("h16", 15, A, 16), r("e1", 0, 15), ALU.max)
        elif k == "k":
            tt(r("src"), r("src"), r("cand"), ALU.max)
        elif k == "l":
            n, arr = (24 if whole_out else 48), "arr%d" % (1 + t)
            cp(r("srcu", at, at + 72), r("src"))
            send(r("srcu", at, at + n), r("lland", 48 * (t - 1), 48 * (t - 1) + n), arr, "sent", False)
            arrives([r("lland", 48 * (t - 1), 48 * t)], arr, 1)
        elif k == "r":
            relu(q, r("h1p", a * HP + 16 + C, (a + 1) * HP), 4 + a, 2.0 ** -6)
        elif k == "z":
            tt(r("z1", a, 4 * A, 4), r("h1p", a * HP, (a + 1) * HP), r("zb", a, 4 * A, 4), ALU.add,
               off=r("offb", 0, 15))
        elif k == "t":
            relu(q, r("t0", a, 4 * A, 4), 4 + a, 2.0 ** -5)
        elif k == "u":
            quant("s", sent_t(t - 1, 0), A, r("t0"))
            if whole_in:
                send_pair(sent_t(t - 1, 0), A, "arr%d" % (3 + t), (sent_h1(t), HR))
                lo, hi = sent_h1(t) + HR, sent_h1(t) + C
                arrives([r("ql", lo, hi), r("cl", lo, hi)], "arr%d" % (7 + t), 2)
            else:
                send_pair(sent_t(t - 1, 0), A, "arr%d" % (3 + t), land(t))
        elif k == "W":
            quant("z1", 0, A, r("z1"))
            for b in range(4):
                mm(b, "w", 128 * b, "z1", 0, A)
        elif k == "R":
            relu(q, r("t1", a, 4 * A, 4) if t < R else r("h2p", a * PL + sec, a * PL + sec + A), a, 2.0 ** -5)
        elif k == "E":
            if q == "s":
                planes("h2p", PL, sec, r("t1"), A)
            else:
                for b in (2 * t - 2, 2 * t - 1):
                    pool_copy(r("h2p", b * PL, b * PL + C), r("h2", b, 4 * C, 4), C)
        elif k == "T":
            quant("s", sent_t(t - 1, 1), A, r("t1"))
            send_pair(sent_t(t - 1, 1), A, "arr%d" % (5 + t), (sent_t(t - 1, 1), A))
        elif k == "H":
            move(q, r("h1", a, 4 * C, 4), r("h1p", a * HP, (a + 1) * HP), off=r("srcu", at + 48, at + 72), scale=2.0)
        elif k == "h":
            quant("s", sent_h1(t), C, r("h1"))
        elif k == "I":
            lo, hi = hruns[a // 4]
            move(q, r("h1", 4 * lo + a % 4, 4 * hi, 4), r("h1p", a % 4 * HP, (a % 4 + 1) * HP),
                 off=r("srcu", at + 48 + lo // 16, at + 48 + hi // 16), scale=2.0)
        elif k == "i":
            lo, hi = hruns[a]
            quant("s", sent_h1(t) + lo, hi - lo, r("h1", 4 * lo, 4 * hi))
        elif k == "j":
            lo, hi = hruns[a]
            send_pair(sent_h1(t) + lo, hi - lo, "arr%d" % (3 + t + 4 * a),
                      (sent_h1(t) + lo, hi - lo) if whole_in else None if a else land(t))
        elif k == "J":
            lo, hi = hruns[a]
            for b in range(4):
                mm(4 + b, "e", 128 * b, "l", sent_h1(t) + lo, hi - lo)
        elif k == "K":
            lo, hi = hruns[a // 4]
            move(q, log(0, t, a % 4, lo, hi), bank(4 + a % 4, hi - lo))
        elif k == "U":
            lo, hi = hruns[a]
            add_log(t, lo, hi)
            quant("g0", lo, hi - lo, log(0, t, None, lo, hi))
        elif k == "P":
            mm(PB[near_out], "up", 0, "s", sent_h1(t), C)
        elif k == "p":
            move(q, r("p1"), bank(PB[near_out], C))
        elif k == "v":
            hold_pattern(0)
        elif k == "w":
            name, pattern, own = (("a2", r("mod4"), col(3)), ("a3", r("modi", 0, A), col(1)))[a]
            ts(r(name), pattern, own, ALU.is_gt, FAR + STEP, ALU.mult)
        elif k == "N":
            for a in range(early, 4):
                act(r("h1p", a * HP + 16, a * HP + 16 + C), r("h1", a, 4 * C, 4), ACT.Copy, scale=0.5)
        elif k == "D":
            lo, n = (0, C) if first else land(t)
            if a:
                lo, n = (C + runs[a - 1][0], runs[a - 1][1] - runs[a - 1][0]) if first else (sent_t(t - 1, 1), A)
            for b in range(4):
                mm(((4, 5, 6, 7), (0, 1, 2, 3), (5, 6, 7, 0))[a][b], "e", 128 * b, "l", lo, n)
        elif k == "C":
            if first or whole_in:
                move(q, log(0, t, a), bank(4 + a, C))
            else:
                move(q, r("gp0", a * PL + sec, a * PL + sec + A), bank(4 + a, A))
        elif k == "G":
            move(q, log(0, t, a), r("gp0", a * PL, a * PL + sec + A), off=r("lland", 48 * t - 24, 48 * t))
        elif k == "Q":
            add_log(t, 0, C)
            quant("g0", 0, C, log(0, t))
        elif k == "S":
            mm(4, "up", 0, "g0", 0, C)
        elif k == "m":
            tt(r("mm"), bank(4, C), r("p1"), ALU.max)
        elif k == "n":
            for b in range(0 if whole_in else 4):
                pool_copy(r("gp0", b * PL, b * PL + C), log(0, 0, b), C)
        elif k == "c":
            if first:
                lo, hi = runs[a // 4]
                move(q, log(1, 0, a % 4, lo, hi), bank((0, 1, 2, 3, 5, 6, 7, 0)[a], hi - lo))
            else:
                move(q, r("gp1", a * PL + sec, a * PL + sec + A), bank(a, A))
        elif k in "ab" and t < R:
            lo, hi = runs[k == "b"]
            move(q, log(1, t, a, lo, hi), r("gp1", a * PL, a * PL + sec + A),
                 off=r("lland", 48 * (t - 1) + lo // 16, 48 * (t - 1) + hi // 16))
        elif k == "q" and t < R:
            quant("g1", lo, hi - lo, log(1, t, None, lo, hi))
            mm(sb[a], "up", 0, "g1", lo, hi - lo)
        elif k == "f":
            s0, s1 = bank(4, hi - lo, lo), bank(sb[a], hi - lo)
            tt(r("nn", lo, hi), s1, r("p0", lo, hi), ALU.max)
            tt(r("fl", 4 + C + lo, 4 + C + hi), s1, r("mm", lo, hi), ALU.is_gt)
            tt(r("fl", 2 + lo, 2 + hi), s0, r("nn", lo, hi), ALU.is_ge)
        elif k == "L":
            wrote = dma("y", T.ol[:], T.olb[0:128:16, :], [r("olb")], [])
            slots_out(R - 1)
            dma("g", T.ol[:], T.ola[0:128:16, :], [r("ola")], [], [wrote], accum_op=ALU.add)
        elif k == "F":
            cp(r("offf"), r("src", 0, 24))
        elif k in "ab":
            lo, hi = last[k == "b"]
            move(q, r("h2f", 4 * lo + a, 4 * hi, 4), r("h2p", a * PL, (a + 1) * PL), off=r("offf", lo // 16, hi // 16))
        elif k == "q":
            quant("f", lo, hi - lo, r("h2f", 4 * lo, 4 * hi))
            mm(4 + a, "v", 0, "f", lo, hi - lo)
            dma("y", T.oc[:, 4 * lo:4 * hi], T.qf[:, lo:hi].bitcast(dt.uint8), [r("qf", lo, hi)], [])
        elif k == "y":
            move(q, r("yb", lo, hi), bank(4 + a, hi - lo))
            dma("ys"[a], T.y[:, lo:hi], ap(r("yb", lo, hi)), [r("yb", lo, hi)], [])
        elif k == "o":
            dma(q, T.osc[4 * a:4 * a + 4, 0:C], T.cf[32 * a:32 * a + 4, 0:C], [r("cf")], [])

    for word in OPEN.split():
        step(word, 0)
    for t in range(R):
        m0, lw = "m%d" % t, "lw%d" % t

        act(r("junk"), r("fl", 2, 2 + C), ACT.Identity, scale=-2.0, acc=r("n0"))
        act(r("sg"), r("icat"), ACT.Sign, scale=2.0, bias=r("n0"))
        act(r("src", 48, 72), r("lane"), ACT.Identity, bias=16.0)
        act(r("sgo"), r("ramph"), ACT.Sign, scale=2.0, bias=r("n0"))
        act(r("olb", A * t, A * t + A), r("sgo"), ACT.Copy, scale=192.0)
        for k in (1, 0):
            lo = 2 + (C + 2) * k
            scan(r("cnt", C * k, C * k + C), r("fl", lo, lo + C), r("fl", lo - 1, lo - 1 + C), float(K),
                 ALU.add, ALU.add)
        for k in (1, 0):
            scan(r("held", C * k, C * k + C), r("a1", C * k, C * k + C), r("cnt", C * k, C * k + C), 0.0,
                 ALU.max, ALU.min)
        mine = [r("held", 15, C, 16), r("v1")]
        ts(mine[1], r("held", C + 15, 2 * C, 16), r("n0"), ALU.subtract, K + 2.0 * A, ALU.min)
        for k in range(2):
            ts(r("pair", 48 * k, 48 * k + 48, 2), mine[k], 0.5, ALU.add)
        for k in range(2):
            tt(r("keep", 48 * k + 1, 48 * k + 48, 2), mine[k], r("pair", 48 * k, 48 * k + 48, 2), ALU.is_lt)
        if t == 0:
            step("vw0", 0)
        if t == 1:
            quant("v", 0, 128, r("vb"))
        scan(r("yw"), r("keep"), r("pair"), 0.0, ALU.mult, ALU.max)
        if t == 0:
            step("vw1", 0)
        tt(r("ow"), r("yw", 1, 48, 2), r("yw", 49, 96, 2), ALU.max)
        cp(r("offs"), r("ow"))
        tt(r("e1"), r("tc"), r("sg"), ALU.mult)
        if t:
            slots_out(t - 1)
        else:
            act(r("a2"), r("a2"), ACT.Identity, bias=-FAR)
            act(r("a3"), r("a3"), ACT.Identity, bias=-FAR)
        if t == R - 1:
            act(r("cand2"), r("ow"), ACT.Sign, bias=-float(K))
            act(r("cand2"), r("cand2"), ACT.Relu, scale=float(2 * SEC))
        at = tsec(t % 2) - 1.0 - K // 2
        act(r("cand", 0, 24), r("ow"), ACT.Identity, scale=0.5, bias=at)
        if t < R - 1:
            act(r("cand", 24, 48), r("yw", 1, 48, 2), ACT.Identity, scale=0.5, bias=at)
            act(r("cand", 48, 72), r("yw", 1, 48, 2), ACT.Identity, scale=0.5, bias=15.0 + C - K // 2)
        if t == 0:
            planes("gp1", PL, 0, log(1, 0), C)
        else:
            planes("h1p", HP, 16, r("h1"), C, 0.5)
        op("v", lambda: g.vector.tensor_copy(ap(r(lw)).indirect(ap(r("offs"))), ap(r("val"))),
           [r("val"), r("offs")], [r(lw)])
        if t < R - 1:
            step("vk", t + 1)
        else:
            tt(r("cand", 0, 24), r("cand", 0, 24), r("cand2"), ALU.add)
        scan(r("h4"), r("a2"), slots(t), 0.0, ALU.add, ALU.max)
        if t < R - 1:
            step("vl", t + 1)
        else:
            tt(r("src", 0, 24), r("src", 0, 24), r("cand", 0, 24), ALU.max)
        ts(r("offz"), r("h4", 3, A, 4), 4.0, ALU.mult, col(4), ALU.add)
        scan(r("h16"), r("a3"), slots(t), 0.0, ALU.add, ALU.max)

        move("s", r("z0", 0, 16 * CZ), r(m0), off=r("offz", 0, CZ), scale=0.5)
        began = move("v", r("z0", 16 * CZ), r(m0), off=r("offz", CZ, 60), scale=0.5)
        if t < R - 1:
            ahead = r("m%d" % (t + 1), 16)
            dma("y", ap(ahead), T.x[:, 0:4 * C], [], [ahead], [began])
        step("vx0", t + 1)
        quant("z0", 0, A, r("z0"))
        step("vx1", t + 1)
        for a in range(4):
            mm(4 + a, "w", 128 * a, "z0", 0, A)


        for word in ((RY if near_out else RX) if t < R - 1 else LAST + " " + END).split():
            step(word, t + 1)
    stores = ["d%d" % i for i in range(dmas[0] - 8, dmas[0])]
    late = ["nt", "ns", "nv"] + stores
    for s in [s for s in total if s not in late] + late:
        if waited["g"].get(s, 0) < total[s] or s in ("sent0", "sent") or s.startswith("arr"):
            g.wait_ge(T.sem[s], total[s])
